import numpy as np, ml_dtypes
CORES = [3,7,11,15,131,135,139,143]
N = 8
import mx_ref
BF = ml_dtypes.bfloat16
def gentries(a):
    return np.ascontiguousarray(a.reshape(8, 16, -1).transpose(0, 2, 1)).reshape(8, -1)
def gtable(e):
    e = np.asarray(e); return np.ascontiguousarray(e.reshape(8, -1, 16).transpose(0, 2, 1)).reshape(128, -1).astype(np.int32)
def gcols(t, e):
    v = np.concatenate([t.reshape(8, 16, -1, 4), np.zeros((8, 16, 1, 4), BF)], axis=2)
    return np.ascontiguousarray(np.stack([v[g][:, e[g]] for g in range(8)])).reshape(128, -1)
def tile(rs):
    return np.stack(rs, axis=2).reshape(128, -1).astype(BF)
def pick(q, e):
    c = np.concatenate([q[0].reshape(128, -1, 4), np.zeros((128, 1, 4), np.uint8)], axis=1); s = np.concatenate([q[1], np.ones((16, 1), np.uint8)], axis=1)
    return (np.ascontiguousarray(c[:, e].reshape(128, -1)), np.ascontiguousarray(s[:, e]))
def join(*qs):
    return (np.concatenate([q[0] for q in qs], axis=1), np.concatenate([q[1] for q in qs], axis=1))
def put(q, e, v):
    c, s = q[0].reshape(128, -1, 4).copy(), q[1].copy(); c[:, e] = v[0].reshape(128, -1, 4); s[:, e] = v[1]
    return (c.reshape(128, -1), s)
def pk(c, s):
    return (np.ascontiguousarray(c), mx_ref.live(s))
def emit(q):
    return q[0], q[1]
def packed(v, rng):
    q = [mx_ref.quantize(np.ascontiguousarray(v[r])) for r in range(N)]
    return np.stack([a for a, b in q]), np.stack([mx_ref.plane(b, rng) for a, b in q])
def values_of_codes():
    e, c = np.zeros((128, 128, 4), np.float32), np.zeros((128, 2, 4), np.uint8)
    e[np.arange(128), np.arange(128), 0] = 1
    c[:127, :, 0] = np.arange(256).reshape(2, 128).T[:127]
    return mx_ref.matmul(mx_ref.quantize(e.reshape(128, 512).astype(BF)), (c.reshape(128, 8), np.full((16, 2), 127, np.uint8))).T.reshape(-1).astype(np.float64)
CODE_VALUE, SCALE_VALUE = values_of_codes(), 2.0 ** (np.arange(256) - 127.0)
def decode(q):
    return (CODE_VALUE[q[0]].reshape(16, 8, -1, 4) * SCALE_VALUE[q[1]][:, None, :, None] + 0.0).reshape(128, -1).astype(np.float32)
def f(rng, *shape):
    return mx_ref.flush((rng.standard_normal(shape, dtype=np.float32) * np.exp2(rng.integers(-2, 3, shape[:-1] + (1,)))).astype(BF))
def wide(rng, *shape, cols=0):
    v = rng.standard_normal(shape, dtype=np.float32) * np.exp2(rng.integers(-12, 13, shape)).astype(np.float32)
    if cols: v *= np.repeat(np.exp2(rng.integers(-cols, cols + 1, shape[:-2] + (1, shape[-1] // 4))) * (rng.random(shape[:-2] + (1, shape[-1] // 4)) > 0.0625), 4, axis=-1).astype(np.float32)
    return mx_ref.flush(v.astype(BF))
C, B, R = 256, 7, 3
K = 1 << B
def items(p):
    return np.sum((p.reshape(8, 16, -1)[:, :B] + np.float32(0.0) < 0) * (1 << np.arange(B))[:, None], axis=1)
def distances(a, n):
    last = K - 1 - np.argsort(a, axis=2)
    d = np.zeros((N, 8, C), np.int64)
    for j in range(C):
        i = n[:, :, j:j + 1]
        d[:, :, j] = np.sum(last > np.take_along_axis(last, i, axis=2), axis=2)
        np.put_along_axis(last, i, K + j, axis=2)
    return d, last
def big(v):
    v = v.astype(np.float32)
    v[np.abs(v) < np.float32(2.0 ** -16)] = 0
    return v.astype(BF)
def fronts(rng):
    return np.argsort(rng.random((N, 8, K)), axis=2)
def stored(a):
    return np.stack([gtable(e) for e in a])
def numbers_of(rng):
    return {"x": big(f(rng, N, 128, 4 * C)), "h": big(f(rng, N, 128, 4 * K)), "nm": stored(fronts(rng)), "u": np.array(f(rng, N, 128, 512)), "v": np.array(f(rng, N, 128, 512))}
def layers(w, rng):
    c, p = packed(np.ascontiguousarray(w).reshape(N, 128, 2048), rng)
    return {"wc": c, "ws": p}
def weights(rng, q=-1):
    w = np.array(f(rng, N, 128, 2048)).reshape(N, 128, 4, 128, 4)
    if q >= 0:
        w[:, 16 * q:16 * q + 16] = 0
        for i in range(16 * q, 16 * q + 16):
            w[:, :, :, i] = 0
            for b in range(4): w[:, i, b, i, b] = 64
    return layers(w, rng)
def seven(c, rng):
    j = np.arange(C)
    a = j % (2 * K)
    return [c[j % K], c[np.minimum(a, 2 * K - 1 - a)], c[rng.integers(0, 3, C)], c[8 * j // C], np.full(C, K - 1), rng.integers(0, K, C), rng.integers(0, K // 2, C)]
def setup_inputs(rng):
    return {**numbers_of(rng), **weights(rng)}
def setup_inputs_traces(rng):
    d, nm = numbers_of(rng), fronts(rng)
    q = int(rng.integers(8))
    size = np.exp2(np.array([-29.0, -12.0, 0.0, 10.0])[rng.permutation(N) % 4])
    x, h = d["x"].reshape(N, 128, C, 4), d["h"].reshape(N, 128, K, 4)
    x[:, 16 * q:16 * q + 16] = 0
    h[:, 16 * q:16 * q + 16] = 0
    u = d["u"].reshape(N, 128, 8, 16, 4)
    u[:, :, :, :B] = 0
    rest = np.delete(np.arange(8), q)
    k = np.arange(7 * B)
    for r in range(N):
        n = np.zeros((8, C), np.int64)
        for i, g in enumerate(rng.permutation(rest)): n[g] = seven(nm[r, g][::-1], rng)[i]
        digit = (n[rest][:, None] >> np.arange(B)[:, None]) & 1
        mark = np.zeros((64, C))
        mark[:7 * B] = np.where(digit == 1, -1, rng.integers(0, 2, digit.shape)).reshape(7 * B, C) * size[r]
        mark[:, C - 1] = 0
        x[r, 16 * q:16 * q + 16] = mark.reshape(16, 4, C).transpose(0, 2, 1).astype(np.float32).astype(BF)
        u[r, 16 * q + k // 4, rest[k // B], k % B, k % 4] = 2.0 ** -30 if size[r] < 2.0 ** -20 else 1.0
    return {"x": x.reshape(N, 128, 4 * C), "h": h.reshape(N, 128, 4 * K), "nm": stored(nm), "u": u.reshape(N, 128, 512), "v": d["v"], **weights(rng, q)}
def setup_inputs_copies(rng):
    d = setup_inputs(rng)
    o = rng.permutation(N)
    x = d["x"].reshape(N, 128, C, 4)
    for r in range(N): x[r] = x[r][:, rng.integers(0, 1 + 2 * o[r], C)]
    x[o == 1] = 0
    d["x"] = x.reshape(N, 128, 4 * C)
    return d
def setup_inputs_huge(rng):
    d = numbers_of(rng)
    o = rng.permutation(N)
    s = rng.choice([-1.0, 1.0], (N, 8, C))
    s[o == 0] = -1
    s[o == 1] = 1
    x = 2.0 ** 30 * (0.75 + 0.25 * rng.random((N, 128, C, 4))) * np.tile(s, (1, 16, 1))[:, :, :, None]
    h = 2.0 ** 28 * (0.75 + 0.25 * rng.random((N, 128, 4 * K))) * rng.choice([-1.0, 1.0], (N, 128, 4 * K))
    on = (np.arange(128)[:, None, None] % 8 == np.argsort(rng.random((8, 8)), axis=1)[:, :B]) | (o < 2)[:, None, None, None]
    u = d["u"].reshape(N, 128, 8, 16, 4)
    u[:, :, :, :B] = (2.0 ** 30 * (0.75 + 0.25 * rng.random((N, 128, 8, B, 4))) * on[:, :, :, :, None]).astype(np.float32).astype(BF)
    w = np.zeros((N, 128, 4, 128, 4), np.float32)
    i = np.arange(128)
    for b in range(4): w[:, i, b, i, b] = 32
    return {"x": x.astype(np.float32).reshape(N, 128, 4 * C).astype(BF), "h": h.astype(np.float32).astype(BF), "nm": d["nm"], "u": u.reshape(N, 128, 512), "v": d["v"], **layers(w.astype(BF), rng)}
def setup_inputs_spread(rng):
    d = setup_inputs(rng)
    d["x"] = big(wide(rng, N, 128, 4 * C, cols=6))
    d["h"] = big(wide(rng, N, 128, 4 * K, cols=6))
    return d
def check_inputs(d):
    b = []
    for k in ("x", "h", "u", "v"):
        a = np.abs(d[k].astype(np.float32))
        if not (np.isfinite(a).all() and ((a == 0) | (a >= 2.0 ** -30) & (a <= 2.0 ** 30)).all()): b.append("a value of " + k)
    if any((np.sort(gentries(d["nm"][r]), axis=1) != np.arange(K)).any() for r in range(N)): b.append("nm: a group's entries aren't a permutation")
    return b
def reference(x, h, nm, u, v, wc, ws):
    qu = [mx_ref.quantize(u[r]) for r in range(N)]
    lay = [pk(wc[r], ws[r]) for r in range(N)]
    qx = [mx_ref.quantize(x[r]) for r in range(N)]
    qf = [mx_ref.quantize(h[r]) for r in range(N)]
    a = np.stack([gentries(nm[r]) for r in range(N)]).astype(np.int64)
    for t in range(R):
        d, last = distances(a, np.stack([items(mx_ref.matmul(qu[r], qx[r])) for r in range(N)]))
        m = np.argsort(-last, axis=2, kind="stable")
        s = np.take_along_axis(last, m, axis=2)
        border = []
        for r in range(N):
            own, front = decode(qx[r]).astype(BF), decode(qf[r]).astype(BF)
            z = ((own.astype(np.float32) + gcols(front, d[r]).astype(np.float32)) * np.float32(0.5)).astype(BF)
            q = mx_ref.quantize(z)
            qx[r] = mx_ref.quantize(tile([mx_ref.matmul(pick(lay[r], np.arange(128 * b, 128 * b + 128)), q) * np.float32(0.03125) for b in range(4)]))
            both = np.concatenate([decode(qx[r]).astype(BF), front], axis=1)
            border.append(mx_ref.quantize(gcols(both, np.where(s[r] >= K, s[r] - K, C + K - 1 - s[r]))))
        qf = [border[(r - 1) % N] for r in range(N)]
        a = np.stack([m[(r - 1) % N] for r in range(N)])
    y, ol = np.zeros((N, 128, C + K), np.float32), np.zeros((N, 8, C + K), np.float32)
    oc, osc = np.zeros((N, 128, 4 * (C + K)), np.uint8), np.zeros((N, 16, C + K), np.uint8)
    for r in range(N):
        q = join(qx[r], qf[r])
        y[r] = mx_ref.matmul(mx_ref.quantize(v[r]), q)
        ol[r] = np.concatenate([d[r], a[r]], axis=1)
        oc[r], osc[r] = emit(q)
    return {"y": y, "ol": ol, "oc": oc, "osc": osc}

@@ -1,0 +1,452 @@
+from concourse.bass import DstId, RemoteDMATransfer
+from concourse.mybir import dt, AluOpType as A, ActivationFunctionType as F, AxisListType
+
+C, K, R = 256, 128, 3
+MS = 10
+HALF = 0.5
+
+
+def off(m):
+    return 256 + 8 * m * (m - 1)
+
+
+S1, S2 = off(16), off(MS)
+BF, F32, I32, U16, U8, Q8 = "bfloat16", "float32", "int32", "uint16", "uint8", "float8_e4m3fn_x4"
+SCRATCH, TINY = {}, {}
+
+
+def buf(name, n, d=BF, where="sbuf"):
+    SCRATCH[name] = (where, [128, n], d)
+
+
+for _n, _w in (("xin", 1024), ("hin", 512), ("uin", 512), ("vin", 512), ("bits", 1024), ("ctile", 2048), ("ntile", 512),
+               ("zt", 1024), ("yt", 1024), ("blk", 128), ("idn", 128), ("w56", 56), ("r16", 256), ("diag", 256), ("maskb", 256),
+               ("keep", 2176), ("inc", 2176), ("iota", 384), ("plc", 128), ("zeros", 256), ("ones", 384), ("hm", 256), ("hold", 256),
+               ("nmask", 256), ("qq", 2176), ("sc", 2176), ("pl", 256), ("plh", 256), ("vr", 256), ("vm", 256), ("vw", 16), ("lt", S2),
+               ("sc2", S2 + 16), ("junk", 384), ("ltb", 384), ("mn", 128), ("mh", 128), ("es", 512), ("arow", 384), ("gx", 1536)):
+    buf(_n, _w)
+for _n, _w in (("kap", 1), ("pw", 1), ("k2", 1), ("e1", 1), ("e2", 1), ("pe", 1), ("sel1", 1), ("sel2", 1), ("pr", 1), ("base", 32), ("thr", 8),
+               ("thr0", 8), ("t32", 32), ("w1", 16), ("w", 16), ("acc", 16), ("e32", 32), ("dd", 32), ("d", 16), ("accb", 8), ("ct", 8),
+               ("sa_", 8), ("sb_", 8), ("sf_", 8), ("b1", 1), ("b4", 1), ("b645", 1), ("bm1", 1)):
+    TINY[_n] = (sum(w for o, w in TINY.values()), _w)
+buf("tiny", sum(w for o, w in TINY.values()), F32)
+for _n, _w in (("ysb", 384), ("olb", 384), ("iotap", 256)):
+    buf(_n, _w, F32)
+for _n, _w in (("qi", 1), ("qi2", 1), ("il", 16), ("im", 16), ("nmi", 8)):
+    buf(_n, _w, I32)
+for _n, _w in (("lh", 16), ("lm", 16), ("ends", 2), ("ends2", 2), ("nw16", 16), ("v16", 16), ("d16", 16), ("src16", 8), ("la0", 8)):
+    buf(_n, _w, U16)
+for _t in range(R):
+    buf("g%d" % _t, 1536)
+    buf("trw%d" % _t, 384)
+    buf("pt%d" % _t, 128)
+    buf("alive%d" % _t, 384)
+    buf("bt%d" % _t, 512)
+    buf("sa%d" % _t, 8, U16)
+    buf("la%d" % (_t + 1), 8, U16)
+    buf("qb%d" % _t, 128, Q8)
+    buf("sb%d" % _t, 128, U8)
+for _n, _w in (("u", 128), ("v", 128), ("w", 512), ("e", 512), ("n", 128), ("bit", 256), ("z", 256),
+               ("x0", 256), ("x1", 256), ("x2", 256), ("x3", 256), ("f0", 128), ("f1", 128), ("f2", 128), ("f3", 128)):
+    buf("q" + _n, _w, Q8)
+    buf("s" + _n, _w, U8)
+for _n in range(8):
+    buf("p%d" % _n, 512, F32, "psum")
+
+NDMA = 22
+SEMAPHORES = ["cv", "cs", "cp", "cg", "left"] + ["ra%d" % t for t in range(R)] + ["rb%d" % t for t in range(R)] + ["d%d" % i for i in range(NDMA)]
+
+
+def rank_program(g, core, T, topo):
+    rank = T.rank_of(core)
+    if rank is None:
+        return
+    queues = {"V": g.vector, "S": g.scalar, "P": g.tensor, "G": g, "Y": g.sync}
+    semof = {"V": "cv", "S": "cs", "P": "cp", "G": "cg"}
+    count = {"cv": 0, "cs": 0, "cp": 0, "cg": 0}
+    seen = {q: {} for q in queues}
+    hist, dmas, left = {}, [0], [0]
+
+    def wait(q, needs):
+        for s in sorted(needs):
+            if seen[q].get(s, 0) < needs[s]:
+                queues[q].wait_ge(T.sem[s], needs[s])
+                seen[q][s] = needs[s]
+
+    def need_of(q, reads, writes):
+        needs = {}
+        for refs, wr in ((reads, False), (writes, True)):
+            for name, lo, hi in refs:
+                psum = SCRATCH[name][0] == "psum"
+                for l, h, w, q2, s, n in hist.get(name, []):
+                    if l < hi and lo < h and (w or wr or (psum and q2 != q)):
+                        needs[s] = max(needs.get(s, 0), n)
+        return needs
+
+    def note(q, reads, writes, s, n):
+        for name, lo, hi in writes:
+            hist[name] = [r for r in hist.get(name, []) if not (lo <= r[0] and r[1] <= hi)] + [(lo, hi, True, q, s, n)]
+        for name, lo, hi in reads:
+            hist[name] = [r for r in hist.get(name, []) if r[2] or r[3] != q or not (lo <= r[0] and r[1] <= hi)] + [(lo, hi, False, q, s, n)]
+
+    def emit(q, fn, reads, writes):
+        wait(q, need_of(q, reads, writes))
+        s = semof[q]
+        count[s] += 1
+        fn().then_inc(T.sem[s], 1)
+        note(q, reads, writes, s, count[s])
+
+    def dma(q, o, i, reads, writes):
+        wait(q, need_of(q, reads, writes))
+        s = "d%d" % dmas[0]
+        dmas[0] += 1
+        queues[q].dma_start(o, i).then_inc(T.sem[s], 16)
+        note(q + "d", reads, writes, s, 16)
+
+    def v(name, a=0, b=None, st=None):
+        if name in TINY:
+            o, n = TINY[name]
+            return v("tiny", o + a, o + (n if b is None else b), st)
+        b = SCRATCH[name][1][1] if b is None else b
+        view = T[name][:, a:b] if st is None else T[name][:, a:b:st]
+        return view, [(name, a, b)]
+
+    def ps(bank, n):
+        return T["p%d" % bank][:, 0:n], [("p%d" % bank, 0, 512)]
+
+    def ind(win, lst):
+        return win[0].indirect(lst[0]), win[1] + lst[1]
+
+    def tt(o, a, b, op):
+        emit("V", lambda: g.vector.tensor_tensor(o[0], a[0], b[0], op), a[1] + b[1], o[1])
+
+    def ts(o, a, s1, op0, s2=None, op1=None):
+        r, x = list(a[1]), [s1, s2]
+        for i in (0, 1):
+            if isinstance(x[i], tuple):
+                r += x[i][1]
+                x[i] = x[i][0]
+        if op1 is None:
+            emit("V", lambda: g.vector.tensor_scalar(o[0], a[0], x[0], None, op0), r, o[1])
+        else:
+            emit("V", lambda: g.vector.tensor_scalar(o[0], a[0], x[0], x[1], op0, op1), r, o[1])
+
+    def cp(o, a):
+        emit("V", lambda: g.vector.tensor_copy(o[0], a[0]), a[1], o[1])
+
+    def scan(o, d0, d1, init, op0, op1):
+        emit("V", lambda: g.vector.tensor_tensor_scan(o[0], d0[0], d1[0], init, op0, op1), d0[1] + d1[1], o[1])
+
+    def total(o, a):
+        emit("V", lambda: g.vector.tensor_reduce(o[0], a[0], AxisListType.X, A.add), a[1], o[1])
+
+    def fill(o, c):
+        emit("V", lambda: g.vector.memset(o[0], c), [], o[1])
+
+    def act(o, a, func, bias=None, scale=1.0, acc=None):
+        r, w, kw = list(a[1]), list(o[1]), {"scale": scale}
+        if bias is not None:
+            kw["bias"] = bias[0]
+            r += bias[1]
+        if acc is not None:
+            kw["accum_out"] = acc[0]
+            w += acc[1]
+        emit("S", lambda: g.scalar.activation(o[0], a[0], func, **kw), r, w)
+
+    def quant(name, src, n):
+        q, s = v("q" + name, 0, n), v("s" + name, 0, n)
+        emit("V", lambda: g.vector.quantize_mx(q[0], s[0], src[0]), src[1], q[1] + s[1])
+
+    def mm(bank, n, l, la, r):
+        o = ps(bank, n)
+        lq, ls = v("q" + l, la, la + 128), v("s" + l, la, la + 128)
+        rq, rs = v("q" + r, 0, n), v("s" + r, 0, n)
+        emit("P", lambda: g.tensor.matmul_mx(o[0], lq[0], ls[0], rq[0], rs[0], True, True), lq[1] + ls[1] + rq[1] + rs[1], o[1])
+
+    def iota(o, pattern, base=0, cm=0, small=True):
+        if small:
+            emit("G", lambda: g.iota(o[0], pattern, base, cm, allow_small_or_imprecise_dtypes=True), [], o[1])
+        else:
+            emit("G", lambda: g.iota(o[0], pattern, base, cm), [], o[1])
+
+    def keep_where(o, pattern, op, base, cm):
+        emit("G", lambda: g.affine_select(o[0], o[0], pattern, op, 0.0, base, cm), o[1], o[1])
+
+    dma("Y", T.xin[:], T.x[:], [], v("xin")[1])
+    dma("S", T.uin[:], T.u[:], [], v("uin")[1])
+    dma("Y", T.nmi[:], T.nm[:], [], v("nmi")[1])
+    dma("S", T.hin[:], T.h[:], [], v("hin")[1])
+    dma("Y", T.qw[:, 0:512].bitcast(dt.uint8), T.wc[:, 0:2048], [], v("qw")[1])
+    dma("S", T.sw[:], T.ws[:], [], v("sw")[1])
+    dma("Y", T.vin[:], T.v[:], [], v("vin")[1])
+
+    iota(v("qi"), [[0, 1]], 0, 1, small=False)
+    fill(v("w56"), 0.0)
+    fill(v("blk"), 1.0)
+    for i in range(7):
+        fill(v("w56", i, 56, 7), float(2 ** i))
+    fill(v("idn"), HALF)
+    keep_where(v("blk"), [[-16, 8], [0, 16]], A.is_ge, 0, 1)
+    keep_where(v("blk"), [[16, 8], [0, 16]], A.is_ge, 15, -1)
+    keep_where(v("w56"), [[-16, 8], [-1, 7]], A.is_equal, 0, 1)
+    iota(v("r16"), [[0, 16], [1, 16]])
+    keep_where(v("idn"), [[-1, 128]], A.is_equal, 0, 1)
+    iota(v("il"), [[16, 16]], 15, 0, small=False)
+    iota(v("im"), [[1, 16]], 0, 0, small=False)
+    iota(v("iotap"), [[1, 256]])
+    iota(v("base"), [[-16, 2], [16, 16]], 15)
+    iota(v("iota"), [[1, 384]], -128)
+    iota(v("sc2", S2, S2 + 16), [[8, 16]])
+    iota(v("thr0"), [[16, 8]])
+    fill(v("ntile"), 0.0)
+    fill(v("bits"), 0.0)
+    fill(v("b1"), 1.0)
+    emit("V", lambda: g.vector.tensor_scalar(T.qi2[:], T.qi[:], 15, None, A.bitwise_and), v("qi")[1], v("qi2")[1])
+    cp(v("kap"), v("qi2"))
+    total(v("pw"), v("w56"))
+    ts(v("ntile", 0, 512, 4), v("blk"), v("pw"), A.mult)
+    quant("n", v("ntile"), 128)
+    ts(v("diag"), v("r16"), v("kap"), A.is_equal)
+    ts(v("maskb"), v("r16"), v("kap"), A.is_ge, 512.0, A.mult)
+    ts(v("keep", 0, 256), v("r16"), 0.0, A.not_equal)
+    quant("u", v("uin"), 128)
+    tt(v("k2"), v("kap"), v("kap"), A.mult)
+    ts(v("e1"), v("k2"), 8.0, A.mult, 255.0, A.add)
+    ts(v("pe"), v("kap"), 8.0, A.mult, v("e1"), A.add)
+    ts(v("e2"), v("kap"), float(S2), A.add)
+    ts(v("sel1"), v("kap"), 0.5, A.is_ge)
+    ts(v("sel2"), v("kap"), MS - 0.5, A.is_lt, v("sel1"), A.mult)
+    ts(v("pr"), v("pe"), v("e2"), A.subtract, v("sel2"), A.mult)
+    ts(v("ends", 0, 1), v("kap"), 16.0, A.mult, 15.0, A.add)
+    ts(v("ends2", 0, 1), v("kap"), 16.0, A.mult, 15.0, A.add)
+    cp(v("ends", 1, 2), v("pe"))
+    ts(v("ends2", 1, 2), v("pr"), v("e2"), A.add)
+    quant("x0", v("xin"), 256)
+    act(v("keep", 256, 512), v("diag"), F.Identity, bias=v("b1"), scale=0.0)
+    act(v("keep", 512, 768), v("keep", 256, 512), F.Copy)
+    act(v("keep", 768, 1280), v("keep", 256, 768), F.Copy)
+    act(v("keep", 1280, 2176), v("keep", 256, 1152), F.Copy)
+    for m in range(1, 16):
+        act(v("keep", off(m), off(m) + 1), v("diag", 0, 1), F.Copy, scale=0.0)
+
+    def gname(t):
+        return "gx" if t == 0 else "g%d" % (t - 1)
+
+    def decode_x(t, planes):
+        for b in planes:
+            mm(4 + b, 256, "e", 128 * b, "x%d" % t)
+
+    def copy_x(t, planes, q="S"):
+        for b in planes:
+            o, i = v(gname(t), 384 * b, 384 * b + 256), ps(4 + b, 256)
+            if q == "S":
+                act(o, i, F.Copy)
+            else:
+                cp(o, i)
+
+    def decode_f(t):
+        for b in range(4):
+            mm(2 + b % 2, 128, "e", 128 * b, "f%d" % t)
+            act(v("g%d" % t, 384 * b + 256, 384 * b + 384), ps(2 + b % 2, 128), F.Copy)
+
+    def front_of(t, b):
+        return v("g%d" % t, 384 * b + 256, 384 * b + 384)
+
+    def names_in(t):
+        emit("V", lambda: g.vector.tensor_copy(T["pt%d" % t][:, 0:128].indirect(T["la%d" % t][:, 0:8]), T.plc[:]),
+             v("plc")[1] + v("la%d" % t)[1], v("pt%d" % t)[1])
+
+    def names_row(t):
+        act(v("trw%d" % t, 256, 384), ind(v("iotap"), v("la%d" % t)), F.Copy)
+
+    nxt = T.cores[(rank + 1) % len(T.cores)]
+    rid, pid = topo.addr(nxt, core)
+    eng = topo.engines(core, nxt)[:8]
+    names_eng = eng[0:8:2]
+
+    def send_names(t):
+        wait("G", need_of("G", v("sa%d" % t)[1], []))
+        g.remote_dma(T["la%d" % (t + 1)][:], T["sa%d" % t][:], T.sem["ra%d" % t], T.sem.left, pid, rid, sum(1 << e for e in names_eng))
+        left[0] += len(names_eng)
+        hist["la%d" % (t + 1)] = [(0, 8, True, "R", "ra%d" % t, len(names_eng))]
+
+    def send_border(t):
+        qb, qf = T["qb%d" % t], T["qf%d" % (t + 1)]
+        wait("G", need_of("G", v("qb%d" % t)[1] + v("sb%d" % t)[1], []))
+        parts = [(qb[:, 32 * i:32 * i + 32].bitcast(dt.uint8), qf[:, 32 * i:32 * i + 32].bitcast(dt.uint8), eng[2 * i]) for i in range(4)]
+        parts.append((T["sb%d" % t][:, 0:128], T["sf%d" % (t + 1)][:, 0:128], eng[1]))
+        g.remote_dma_fused([RemoteDMATransfer(dst_ids=[DstId(rid=rid, pnc=pid)], dma_engine_mask=1 << e, remote_sem=T.sem["rb%d" % t], src=a, dst=b)
+                            for a, b, e in parts], local_sem=T.sem.left)
+        left[0] += len(parts)
+        for n in ("qf%d", "sf%d"):
+            hist[n % (t + 1)] = [(0, 128, True, "R", "rb%d" % t, len(parts))]
+
+    def border_list_1(t):
+        if t == 0:
+            ts(v("thr"), v("thr0"), v("kap"), A.add, -1.0, A.mult)
+            ts(v("thr"), v("thr"), 127.5, A.add)
+            fill(v("ones"), 1.0)
+            for i in range(R):
+                fill(v("alive%d" % i), 1.0)
+        emit("V", lambda: g.vector.tensor_copy(T["alive%d" % t][:, 0:384].indirect(T.v16[:, 0:16]), T.zeros[:]),
+             v("zeros")[1] + v("v16")[1] + v("alive%d" % t)[1], v("alive%d" % t)[1])
+        scan(v("arow"), v("ones"), v("alive%d" % t), 0.0, A.mult, A.add)
+
+    def border_list_2(t):
+        n = 8 if t < R - 1 else 5
+        for m in range(n):
+            act(v("junk", 0, 384), v("arow"), F.Sign, bias=v("thr", m, m + 1), scale=-1.0, acc=v("accb", m, m + 1))
+        for m in range(n, 8):
+            ts(v("ltb"), v("arow"), v("thr", m, m + 1), A.is_lt, 2.0, A.mult)
+            total(v("ct", m, m + 1), v("ltb"))
+        if n < 8:
+            ts(v("accb", n, 8), v("ct", n, 8), -384.0, A.add)
+        act(v("sa_"), v("accb"), F.Abs, bias=v("b645"), scale=0.5)
+
+    def border_list_3(t):
+        ts(v("sb_"), v("accb"), -128.0, A.is_lt, 256.0, A.mult)
+        tt(v("sf_"), v("sa_"), v("sb_"), A.add)
+        ts(v("src16"), v("sf_"), -0.5, A.add)
+        tt(v("mn"), ind(v("trw%d" % t), v("src16")), v("diag", 0, 128), A.mult)
+        scan(v("mh"), v("keep", 0, 128), v("mn"), 0.0, A.mult, A.add)
+        cp(v("sa%d" % t), v("mh", 15, 128, 16))
+        send_names(t)
+
+    def border_gather(t, b, q):
+        o, i = v("bt%d" % t, b, 512, 4), ind(v("g%d" % t, 384 * b, 384 * b + 384), v("src16"))
+        if q == "S":
+            act(o, i, F.Copy, scale=2.0)
+        else:
+            ts(o, i, 2.0, A.mult)
+
+    def border_send(t):
+        quant("b%d" % t, v("bt%d" % t), 128)
+        send_border(t)
+
+    for t in range(R):
+        tr = "trw%d" % t
+        mm(0, 256, "u", 0, "x%d" % t)
+        if t == 0:
+            fill(v("b4"), 4.0)
+            fill(v("bm1"), -1.0)
+            fill(v("b645"), 64.5)
+            cp(v("lh"), v("il"))
+        ts(v("bits", 0, 1024, 4), ps(0, 256), 0.0, A.is_lt)
+        quant("bit", v("bits"), 256)
+        if t > 0:
+            decode_x(t, (0, 1))
+        mm(1, 256, "n", 0, "bit")
+        if t == 0:
+            fill(v("ctile"), 0.0)
+        else:
+            decode_x(t, (2, 3))
+            copy_x(t, (0, 1))
+        tt(v("hm"), ps(1, 256), v("diag"), A.mult)
+        tt(v("nmask"), ps(1, 256), v("maskb"), A.add)
+        act(v(tr, 0, 256), ps(1, 256), F.Copy)
+        scan(v("hold"), v("keep", 0, 256), v("hm"), 0.0, A.mult, A.add)
+        cp(v("nw16"), v("hold", 15, 256, 16))
+        tt(v("qq", 0, 256), ind(v("hold"), v("lh")), v("nmask"), A.not_equal)
+        if t == 0:
+            act(v("inc"), v("keep"), F.Identity, bias=v("b4"), scale=1.0 / 512 - 4.0)
+            act(v("base"), v("base"), F.Copy, scale=1.0 / 512)
+            for b in range(4):
+                act(v("ctile", 512 * b + b, 512 * b + 512, 4), v("idn"), F.Copy)
+            act(v("zeros"), v("diag"), F.Copy, scale=0.0)
+            ts(v("plc"), v("iotap", 0, 128), 1.0 / 512, A.mult, 1.0 / 512, A.add)
+            cp(v("la0"), v("nmi"))
+            names_in(0)
+            cp(v("lm"), v("im"))
+            fill(v("e32"), 0.0)
+        else:
+            border_list_3(t - 1)
+            copy_x(t, (2, 3))
+            for b in range(4):
+                border_gather(t - 1, b, "S")
+        for m in range(1, 16):
+            ts(v("qq", off(m), off(m) + 16 * m), v(tr, 0, 16 * m), v("hold", 16 * m + 15, 16 * m + 16), A.not_equal)
+        if t == 0:
+            fill(v("base", 16, 17), -4.0)
+            quant("f0", v("hin"), 128)
+            quant("e", v("ctile"), 512)
+            decode_x(0, range(4))
+        scan(v("sc"), v("inc"), v("qq"), 4.0, A.add, A.min)
+        tt(v("t32"), ind(v("sc"), v("ends")), v("base"), A.subtract)
+        tt(v("w1"), v("t32", 0, 16), v("t32", 16, 32), A.min)
+        if t > 0:
+            border_send(t - 1)
+            names_in(t)
+        tt(v("pl"), ind(v("pt%d" % t), v("nw16")), v("diag"), A.mult)
+        scan(v("plh"), v("keep", 0, 256), v("pl"), 0.0, A.mult, A.add)
+        tt(v("w"), v("w1"), v("plh", 15, 256, 16), A.min)
+        ts(v("v16"), v("w"), -512.0, A.mult, 128.0, A.add)
+        act(v("vw"), v("w"), F.Copy, scale=-512.0)
+        act(v("vr"), ind(v("iota"), v("v16")), F.Copy)
+        act(v("e32", 0, 16), v("w"), F.Identity, bias=v("bm1"), scale=512.0)
+        for m in range(MS, 16):
+            act(v("junk", 0, 16 * m), v("vr", 0, 16 * m), F.Sign, bias=v("vw", m, m + 1), scale=-1.0, acc=v("acc", m, m + 1))
+        act(v("e32", 16 + MS, 32), v("acc", MS, 16), F.Copy, scale=0.5)
+        tt(v("vm"), ind(v("iota"), v("v16")), v("maskb"), A.add)
+        tt(v("lt", 0, 256), ind(v("vw"), v("lm")), v("vm"), A.is_gt)
+        for m in range(1, MS):
+            ts(v("lt", off(m), off(m) + 16 * m), v("vr", 0, 16 * m), v("vw", m, m + 1), A.is_lt)
+        scan(v("sc2", 0, S2), v("keep", 0, S2), v("lt"), 0.0, A.mult, A.add)
+        tt(v("dd"), ind(v("sc2"), v("ends2")), v("e32"), A.add)
+        tt(v("d"), v("dd", 0, 16), v("dd", 16, 32), A.add)
+        cp(v("d16"), v("d"))
+        if t == 0:
+            copy_x(0, (0, 1))
+        decode_f(t)
+        for b in (2, 3):
+            act(v("es", 256 * (b - 2), 256 * (b - 1)), ind(front_of(t, b), v("d16")), F.Copy)
+        names_row(t)
+        for b in (0, 1):
+            tt(v("zt", b, 1024, 4), ind(front_of(t, b), v("d16")), v(gname(t), 384 * b, 384 * b + 256), A.add)
+        for b in (2, 3):
+            tt(v("zt", b, 1024, 4), v("es", 256 * (b - 2), 256 * (b - 1)), ps(4 + b, 256), A.add)
+        quant("z", v("zt"), 256)
+        for b, bank in enumerate((0, 2, 3, 4)):
+            mm(bank, 256, "w", 128 * b, "z")
+        border_list_1(t)
+        for b, bank in enumerate((0, 2, 3)):
+            act(v("yt", b, 1024, 4), ps(bank, 256), F.Copy, scale=0.03125)
+        ts(v("yt", 3, 1024, 4), ps(4, 256), 0.03125, A.mult)
+        quant("x%d" % (t + 1), v("yt"), 256)
+        border_list_2(t)
+
+    decode_x(R, range(4))
+    border_list_3(R - 1)
+    copy_x(R, (0, 1))
+    copy_x(R, (2, 3), "V")
+    for b in (0, 1):
+        border_gather(R - 1, b, "S")
+    for b in (2, 3):
+        border_gather(R - 1, b, "V")
+    border_send(R - 1)
+    quant("v", v("vin"), 128)
+    mm(1, 256, "v", 0, "x3")
+    act(v("ysb", 0, 256), ps(1, 256), F.Copy)
+    act(v("olb", 0, 256), ind(v("iotap"), v("d16")), F.Copy)
+
+    def stores(a, n, q, s):
+        dma("Y", T.oc[:, 4 * a:4 * (a + n)], T[q][:, 0:n].bitcast(dt.uint8), v(q)[1], [])
+        for k in range(4):
+            dma("Y" if k % 2 else "S", T.osc[4 * k:4 * k + 4, a:a + n], T[s][32 * k:32 * k + 4, 0:n], v(s)[1], [])
+
+    dma("S", T.y[:, 0:256], T.ysb[:, 0:256], v("ysb", 0, 256)[1], [])
+    stores(0, 256, "qx3", "sx3")
+    act(v("olb", 256, 384), ind(v("iotap"), v("la3")), F.Copy)
+    dma("Y", T.ol[:, :], T.olb[0:128:16, :], v("olb")[1], [])
+    mm(2, 128, "v", 0, "f3")
+    cp(v("ysb", 256, 384), ps(2, 128))
+    stores(256, 128, "qf3", "sf3")
+    dma("S", T.y[:, 256:384], T.ysb[:, 256:384], v("ysb", 256, 384)[1], [])
+
+    for s in ("cv", "cs", "cp", "cg"):
+        g.wait_ge(T.sem[s], count[s])
+    for i in range(dmas[0]):
+        g.wait_ge(T.sem["d%d" % i], 16)
+    for i in range(R):
+        g.wait_ge(T.sem["ra%d" % i], len(names_eng))
+        g.wait_ge(T.sem["rb%d" % i], 5)
+    g.wait_ge(T.sem.left, left[0])

@@ -1,8 +1,9 @@
-from concourse.bass import DstId, RemoteDMATransfer
 from concourse.mybir import dt, AluOpType as A, ActivationFunctionType as F, AxisListType
 
 C, K, R = 256, 128, 3
-MS = 10
+MS = 11
+SQ = 14
+NLAST = 5
 HALF = 0.5
 
 
@@ -19,22 +20,22 @@ def buf(name, n, d=BF, where="sbuf"):
     SCRATCH[name] = (where, [128, n], d)
 
 
-for _n, _w in (("xin", 1024), ("hin", 512), ("uin", 512), ("vin", 512), ("bits", 1024), ("ctile", 2048), ("ntile", 512),
+for _n, _w in (("xin", 1024), ("hin", 512), ("uin", 512), ("vin", 512), ("bits", 512), ("ctile", 2048), ("ntile", 1024),
                ("zt", 1024), ("yt", 1024), ("blk", 128), ("idn", 128), ("w56", 56), ("r16", 256), ("diag", 256), ("maskb", 256),
-               ("keep", 2176), ("inc", 2176), ("iota", 384), ("plc", 128), ("zeros", 256), ("ones", 384), ("hm", 256), ("hold", 256),
-               ("nmask", 256), ("qq", 2176), ("sc", 2176), ("pl", 256), ("plh", 256), ("vr", 256), ("vm", 256), ("vw", 16), ("lt", S2),
-               ("sc2", S2 + 16), ("junk", 384), ("ltb", 384), ("mn", 128), ("mh", 128), ("es", 512), ("arow", 384), ("gx", 1536)):
+               ("keep", 2176), ("inc", 2176), ("iota", 384), ("plc", 128), ("plcr", 128), ("zeros", 256), ("ones", 384), ("hm", 256),
+               ("hold", 256), ("nmask", 256), ("qq", 2176), ("sc", 2176), ("pl", 256), ("plh", 256), ("vr", 256), ("vm", 256), ("vw", 16),
+               ("lt", S2), ("sc2", S2 + 16), ("junk", 1536), ("ltb", 272), ("mn", 128), ("mh", 128), ("es", 512), ("arow", 384), ("gx", 1536)):
     buf(_n, _w)
 for _n, _w in (("kap", 1), ("pw", 1), ("k2", 1), ("e1", 1), ("e2", 1), ("pe", 1), ("sel1", 1), ("sel2", 1), ("pr", 1), ("base", 32), ("thr", 8),
-               ("thr0", 8), ("t32", 32), ("w1", 16), ("w", 16), ("acc", 16), ("e32", 32), ("dd", 32), ("d", 16), ("accb", 8), ("ct", 8),
-               ("sa_", 8), ("sb_", 8), ("sf_", 8), ("b1", 1), ("b4", 1), ("b645", 1), ("bm1", 1)):
+               ("thr0", 8), ("thrl", 8), ("t32", 32), ("w1", 16), ("w", 16), ("acc", 16), ("e32", 32), ("dd", 16), ("d", 16), ("accb", 8), ("ct", 8),
+               ("sa_", 8), ("sb_", 8), ("sc_", 8), ("sf_", 8), ("b1", 1), ("b4", 1), ("c2", 8), ("c2l", 8), ("b127", 1), ("bm1", 1)):
     TINY[_n] = (sum(w for o, w in TINY.values()), _w)
 buf("tiny", sum(w for o, w in TINY.values()), F32)
 for _n, _w in (("ysb", 384), ("olb", 384), ("iotap", 256)):
     buf(_n, _w, F32)
 for _n, _w in (("qi", 1), ("qi2", 1), ("il", 16), ("im", 16), ("nmi", 8)):
     buf(_n, _w, I32)
-for _n, _w in (("lh", 16), ("lm", 16), ("ends", 2), ("ends2", 2), ("nw16", 16), ("v16", 16), ("d16", 16), ("src16", 8), ("la0", 8)):
+for _n, _w in (("lh", 16), ("lm", 16), ("ends", 2), ("ends2", 1), ("nw16", 16), ("v16", 16), ("d16", 16), ("src16", 8), ("la0", 8)):
     buf(_n, _w, U16)
 for _t in range(R):
     buf("g%d" % _t, 1536)
@@ -46,7 +47,7 @@ for _t in range(R):
     buf("la%d" % (_t + 1), 8, U16)
     buf("qb%d" % _t, 128, Q8)
     buf("sb%d" % _t, 128, U8)
-for _n, _w in (("u", 128), ("v", 128), ("w", 512), ("e", 512), ("n", 128), ("bit", 256), ("z", 256),
+for _n, _w in (("u", 128), ("v", 128), ("w", 512), ("e", 512), ("n", 256), ("bit", 128), ("z", 256),
                ("x0", 256), ("x1", 256), ("x2", 256), ("x3", 256), ("f0", 128), ("f1", 128), ("f2", 128), ("f3", 128)):
     buf("q" + _n, _w, Q8)
     buf("s" + _n, _w, U8)
@@ -65,7 +66,7 @@ def rank_program(g, core, T, topo):
     semof = {"V": "cv", "S": "cs", "P": "cp", "G": "cg"}
     count = {"cv": 0, "cs": 0, "cp": 0, "cg": 0}
     seen = {q: {} for q in queues}
-    hist, dmas, left = {}, [0], [0]
+    hist, dmas, left, turn = {}, [0], [0], [0]
 
     def wait(q, needs):
         for s in sorted(needs):
@@ -111,8 +112,8 @@ def rank_program(g, core, T, topo):
         view = T[name][:, a:b] if st is None else T[name][:, a:b:st]
         return view, [(name, a, b)]
 
-    def ps(bank, n):
-        return T["p%d" % bank][:, 0:n], [("p%d" % bank, 0, 512)]
+    def ps(bank, n, a=0):
+        return T["p%d" % bank][:, a:a + n], [("p%d" % bank, 0, 512)]
 
     def ind(win, lst):
         return win[0].indirect(lst[0]), win[1] + lst[1]
@@ -153,14 +154,14 @@ def rank_program(g, core, T, topo):
             w += acc[1]
         emit("S", lambda: g.scalar.activation(o[0], a[0], func, **kw), r, w)
 
-    def quant(name, src, n):
-        q, s = v("q" + name, 0, n), v("s" + name, 0, n)
+    def quant(name, src, n, a=0):
+        q, s = v("q" + name, a, a + n), v("s" + name, a, a + n)
         emit("V", lambda: g.vector.quantize_mx(q[0], s[0], src[0]), src[1], q[1] + s[1])
 
-    def mm(bank, n, l, la, r):
+    def mm(bank, n, l, la, r, ra=0):
         o = ps(bank, n)
         lq, ls = v("q" + l, la, la + 128), v("s" + l, la, la + 128)
-        rq, rs = v("q" + r, 0, n), v("s" + r, 0, n)
+        rq, rs = v("q" + r, ra, ra + n), v("s" + r, ra, ra + n)
         emit("P", lambda: g.tensor.matmul_mx(o[0], lq[0], ls[0], rq[0], rs[0], True, True), lq[1] + ls[1] + rq[1] + rs[1], o[1])
 
     def iota(o, pattern, base=0, cm=0, small=True):
@@ -198,6 +199,8 @@ def rank_program(g, core, T, topo):
     iota(v("iota"), [[1, 384]], -128)
     iota(v("sc2", S2, S2 + 16), [[8, 16]])
     iota(v("thr0"), [[16, 8]])
+    iota(v("c2"), [[32, 8]], 272)
+    iota(v("c2l"), [[-32, 8]], 496)
     fill(v("ntile"), 0.0)
     fill(v("bits"), 0.0)
     fill(v("b1"), 1.0)
@@ -205,7 +208,8 @@ def rank_program(g, core, T, topo):
     cp(v("kap"), v("qi2"))
     total(v("pw"), v("w56"))
     ts(v("ntile", 0, 512, 4), v("blk"), v("pw"), A.mult)
-    quant("n", v("ntile"), 128)
+    ts(v("ntile", 513, 1024, 4), v("blk"), v("pw"), A.mult)
+    quant("n", v("ntile"), 256)
     ts(v("diag"), v("r16"), v("kap"), A.is_equal)
     ts(v("maskb"), v("r16"), v("kap"), A.is_ge, 512.0, A.mult)
     ts(v("keep", 0, 256), v("r16"), 0.0, A.not_equal)
@@ -218,9 +222,8 @@ def rank_program(g, core, T, topo):
     ts(v("sel2"), v("kap"), MS - 0.5, A.is_lt, v("sel1"), A.mult)
     ts(v("pr"), v("pe"), v("e2"), A.subtract, v("sel2"), A.mult)
     ts(v("ends", 0, 1), v("kap"), 16.0, A.mult, 15.0, A.add)
-    ts(v("ends2", 0, 1), v("kap"), 16.0, A.mult, 15.0, A.add)
     cp(v("ends", 1, 2), v("pe"))
-    ts(v("ends2", 1, 2), v("pr"), v("e2"), A.add)
+    ts(v("ends2"), v("pr"), v("e2"), A.add)
     quant("x0", v("xin"), 256)
     act(v("keep", 256, 512), v("diag"), F.Identity, bias=v("b1"), scale=0.0)
     act(v("keep", 512, 768), v("keep", 256, 512), F.Copy)
@@ -229,8 +232,11 @@ def rank_program(g, core, T, topo):
     for m in range(1, 16):
         act(v("keep", off(m), off(m) + 1), v("diag", 0, 1), F.Copy, scale=0.0)
 
-    def gname(t):
-        return "gx" if t == 0 else "g%d" % (t - 1)
+    def x_of(t, b, a=0, e=256):
+        return v("gx" if t == 0 else "g%d" % (t - 1), 384 * b + 128 + a, 384 * b + 128 + e)
+
+    def front_of(t, b):
+        return v("g%d" % t, 384 * b, 384 * b + 128)
 
     def decode_x(t, planes):
         for b in planes:
@@ -238,53 +244,49 @@ def rank_program(g, core, T, topo):
 
     def copy_x(t, planes, q="S"):
         for b in planes:
-            o, i = v(gname(t), 384 * b, 384 * b + 256), ps(4 + b, 256)
             if q == "S":
-                act(o, i, F.Copy)
+                act(x_of(t, b), ps(4 + b, 256), F.Copy)
             else:
-                cp(o, i)
+                cp(x_of(t, b), ps(4 + b, 256))
 
     def decode_f(t):
         for b in range(4):
-            mm(2 + b % 2, 128, "e", 128 * b, "f%d" % t)
-            act(v("g%d" % t, 384 * b + 256, 384 * b + 384), ps(2 + b % 2, 128), F.Copy)
-
-    def front_of(t, b):
-        return v("g%d" % t, 384 * b + 256, 384 * b + 384)
+            mm(b, 128, "e", 128 * b, "f%d" % t)
+            act(front_of(t, b), ps(b, 128), F.Copy)
 
     def names_in(t):
-        emit("V", lambda: g.vector.tensor_copy(T["pt%d" % t][:, 0:128].indirect(T["la%d" % t][:, 0:8]), T.plc[:]),
-             v("plc")[1] + v("la%d" % t)[1], v("pt%d" % t)[1])
+        p = "plcr" if t else "plc"
+        emit("V", lambda: g.vector.tensor_copy(T["pt%d" % t][:, 0:128].indirect(T["la%d" % t][:, 0:8]), T[p][:]),
+             v(p)[1] + v("la%d" % t)[1], v("pt%d" % t)[1])
 
     def names_row(t):
-        act(v("trw%d" % t, 256, 384), ind(v("iotap"), v("la%d" % t)), F.Copy)
+        act(v("trw%d" % t, 0, 128), ind(v("iotap", 0, 128), v("la%d" % t)), F.Copy)
 
     nxt = T.cores[(rank + 1) % len(T.cores)]
     rid, pid = topo.addr(nxt, core)
     eng = topo.engines(core, nxt)[:8]
-    names_eng = eng[0:8:2]
+    mask = sum(1 << e for e in eng)
+
+    def send(dst, src, rsem, reads):
+        wait("G", need_of("G", reads, []))
+        g.remote_dma(dst, src, T.sem[rsem], T.sem.left, pid, rid, mask)
+        left[0] += len(eng)
 
     def send_names(t):
-        wait("G", need_of("G", v("sa%d" % t)[1], []))
-        g.remote_dma(T["la%d" % (t + 1)][:], T["sa%d" % t][:], T.sem["ra%d" % t], T.sem.left, pid, rid, sum(1 << e for e in names_eng))
-        left[0] += len(names_eng)
-        hist["la%d" % (t + 1)] = [(0, 8, True, "R", "ra%d" % t, len(names_eng))]
+        send(T["la%d" % (t + 1)][:], T["sa%d" % t][:], "ra%d" % t, v("sa%d" % t)[1])
+        hist["la%d" % (t + 1)] = [(0, 8, True, "R", "ra%d" % t, len(eng))]
 
-    def send_border(t):
-        qb, qf = T["qb%d" % t], T["qf%d" % (t + 1)]
-        wait("G", need_of("G", v("qb%d" % t)[1] + v("sb%d" % t)[1], []))
-        parts = [(qb[:, 32 * i:32 * i + 32].bitcast(dt.uint8), qf[:, 32 * i:32 * i + 32].bitcast(dt.uint8), eng[2 * i]) for i in range(4)]
-        parts.append((T["sb%d" % t][:, 0:128], T["sf%d" % (t + 1)][:, 0:128], eng[1]))
-        g.remote_dma_fused([RemoteDMATransfer(dst_ids=[DstId(rid=rid, pnc=pid)], dma_engine_mask=1 << e, remote_sem=T.sem["rb%d" % t], src=a, dst=b)
-                            for a, b, e in parts], local_sem=T.sem.left)
-        left[0] += len(parts)
+    def border_send(t):
+        quant("b%d" % t, v("bt%d" % t), 128)
+        send(T["qf%d" % (t + 1)][:, 0:128].bitcast(dt.uint8), T["qb%d" % t][:, 0:128].bitcast(dt.uint8), "rb%d" % t, v("qb%d" % t)[1])
+        send(T["sf%d" % (t + 1)][:], T["sb%d" % t][:], "rb%d" % t, v("sb%d" % t)[1])
         for n in ("qf%d", "sf%d"):
-            hist[n % (t + 1)] = [(0, 128, True, "R", "rb%d" % t, len(parts))]
+            hist[n % (t + 1)] = [(0, 128, True, "R", "rb%d" % t, 2 * len(eng))]
 
-    def border_list_1(t):
+    def border_alive(t):
         if t == 0:
-            ts(v("thr"), v("thr0"), v("kap"), A.add, -1.0, A.mult)
-            ts(v("thr"), v("thr"), 127.5, A.add)
+            ts(v("thr"), v("thr0"), v("kap"), A.add, 0.5, A.add)
+            ts(v("thrl"), v("thr"), -1.0, A.mult, 128.0, A.add)
             fill(v("ones"), 1.0)
             for i in range(R):
                 fill(v("alive%d" % i), 1.0)
@@ -292,25 +294,38 @@ def rank_program(g, core, T, topo):
              v("zeros")[1] + v("v16")[1] + v("alive%d" % t)[1], v("alive%d" % t)[1])
         scan(v("arow"), v("ones"), v("alive%d" % t), 0.0, A.mult, A.add)
 
-    def border_list_2(t):
-        n = 8 if t < R - 1 else 5
-        for m in range(n):
-            act(v("junk", 0, 384), v("arow"), F.Sign, bias=v("thr", m, m + 1), scale=-1.0, acc=v("accb", m, m + 1))
-        for m in range(n, 8):
-            ts(v("ltb"), v("arow"), v("thr", m, m + 1), A.is_lt, 2.0, A.mult)
-            total(v("ct", m, m + 1), v("ltb"))
-        if n < 8:
-            ts(v("accb", n, 8), v("ct", n, 8), -384.0, A.add)
-        act(v("sa_"), v("accb"), F.Abs, bias=v("b645"), scale=0.5)
+    def junk(n):
+        turn[0] = (turn[0] + 1) % 4
+        return v("junk", 384 * turn[0], 384 * turn[0] + n)
 
-    def border_list_3(t):
-        ts(v("sb_"), v("accb"), -128.0, A.is_lt, 256.0, A.mult)
-        tt(v("sf_"), v("sa_"), v("sb_"), A.add)
-        ts(v("src16"), v("sf_"), -0.5, A.add)
-        tt(v("mn"), ind(v("trw%d" % t), v("src16")), v("diag", 0, 128), A.mult)
-        scan(v("mh"), v("keep", 0, 128), v("mn"), 0.0, A.mult, A.add)
-        cp(v("sa%d" % t), v("mh", 15, 128, 16))
+    def border_count(t):
+        last = t == R - 1
+        n, thr = (NLAST, "thrl") if last else (8, "thr")
+        for m in range(8):
+            a = 112 - 16 * m if last else 16 * m
+            if m < n:
+                act(junk(272), v("arow", a, a + 272), F.Sign, bias=v(thr, m, m + 1), scale=-1.0, acc=v("accb", m, m + 1))
+            else:
+                ts(v("ltb"), v("arow", a, a + 272), v(thr, m, m + 1), A.is_lt, 2.0, A.mult)
+                total(v("ct", m, m + 1), v("ltb"))
+        if n < 8:
+            ts(v("accb", n, 8), v("ct", n, 8), -272.0, A.add)
+
+    def border_list(t):
+        yield tt(v("sb_"), v("accb"), v("c2l" if t == R - 1 else "c2"), A.add)
+        if t == 0:
+            yield ts(v("sa_"), v("sb_"), 255.5, A.is_ge, 0.5, A.mult)
+            yield ts(v("sc_"), v("sb_"), -0.5, A.mult, 127.0, A.add)
+            yield tt(v("sa_"), v("sa_"), v("sb_"), A.mult)
+            yield tt(v("sf_"), v("sa_"), v("sc_"), A.max)
+            yield cp(v("src16"), v("sf_"))
+        else:
+            yield ts(v("src16"), v("sb_"), 0.5, A.mult)
+        yield tt(v("mn"), ind(v("trw%d" % t), v("src16")), v("diag", 0, 128), A.mult)
+        yield scan(v("mh"), v("keep", 0, 128), v("mn"), 0.0, A.mult, A.add)
+        yield cp(v("sa%d" % t), v("mh", 15, 128, 16))
         send_names(t)
+        yield None
 
     def border_gather(t, b, q):
         o, i = v("bt%d" % t, b, 512, 4), ind(v("g%d" % t, 384 * b, 384 * b + 384), v("src16"))
@@ -319,33 +334,32 @@ def rank_program(g, core, T, topo):
         else:
             ts(o, i, 2.0, A.mult)
 
-    def border_send(t):
-        quant("b%d" % t, v("bt%d" % t), 128)
-        send_border(t)
-
+    mm(0, 128, "u", 0, "x0", 0)
+    mm(1, 128, "u", 0, "x0", 128)
     for t in range(R):
         tr = "trw%d" % t
-        mm(0, 256, "u", 0, "x%d" % t)
         if t == 0:
             fill(v("b4"), 4.0)
             fill(v("bm1"), -1.0)
-            fill(v("b645"), 64.5)
+            fill(v("b127"), 127.0)
             cp(v("lh"), v("il"))
-        ts(v("bits", 0, 1024, 4), ps(0, 256), 0.0, A.is_lt)
-        quant("bit", v("bits"), 256)
+        ts(v("bits", 0, 512, 4), ps(0, 128), 0.0, A.is_lt)
+        ts(v("bits", 1, 512, 4), ps(1, 128), 0.0, A.is_lt)
+        quant("bit", v("bits"), 128)
         if t > 0:
             decode_x(t, (0, 1))
-        mm(1, 256, "n", 0, "bit")
+        mm(2, 128, "n", 0, "bit")
+        mm(3, 128, "n", 128, "bit")
         if t == 0:
             fill(v("ctile"), 0.0)
         else:
             decode_x(t, (2, 3))
-            copy_x(t, (0, 1))
-        tt(v("hm"), ps(1, 256), v("diag"), A.mult)
-        tt(v("nmask"), ps(1, 256), v("maskb"), A.add)
-        act(v(tr, 0, 256), ps(1, 256), F.Copy)
+        for hf in (0, 1):
+            a, e = 128 * hf, 128 * hf + 128
+            tt(v("hm", a, e), ps(2 + hf, 128), v("diag", a, e), A.mult)
+            tt(v("nmask", a, e), ps(2 + hf, 128), v("maskb", a, e), A.add)
+            act(v(tr, 128 + a, 128 + e), ps(2 + hf, 128), F.Copy)
         scan(v("hold"), v("keep", 0, 256), v("hm"), 0.0, A.mult, A.add)
-        cp(v("nw16"), v("hold", 15, 256, 16))
         tt(v("qq", 0, 256), ind(v("hold"), v("lh")), v("nmask"), A.not_equal)
         if t == 0:
             act(v("inc"), v("keep"), F.Identity, bias=v("b4"), scale=1.0 / 512 - 4.0)
@@ -354,29 +368,37 @@ def rank_program(g, core, T, topo):
                 act(v("ctile", 512 * b + b, 512 * b + 512, 4), v("idn"), F.Copy)
             act(v("zeros"), v("diag"), F.Copy, scale=0.0)
             ts(v("plc"), v("iotap", 0, 128), 1.0 / 512, A.mult, 1.0 / 512, A.add)
+            ts(v("plcr"), v("iotap", 0, 128), -1.0 / 512, A.mult, 128.0 / 512, A.add)
             cp(v("la0"), v("nmi"))
             names_in(0)
             cp(v("lm"), v("im"))
-            fill(v("e32"), 0.0)
-        else:
-            border_list_3(t - 1)
-            copy_x(t, (2, 3))
-            for b in range(4):
-                border_gather(t - 1, b, "S")
-        for m in range(1, 16):
-            ts(v("qq", off(m), off(m) + 16 * m), v(tr, 0, 16 * m), v("hold", 16 * m + 15, 16 * m + 16), A.not_equal)
+        for m in range(SQ, 16):
+            act(v("qq", off(m), off(m) + 16 * m), v(tr, 128, 128 + 16 * m), F.Square, bias=v("hold", 16 * m + 15, 16 * m + 16), scale=-1.0)
+        if t > 0:
+            copy_x(t, range(4))
+        steps = border_list(t - 1) if t > 0 else iter(())
+        for m in range(1, SQ):
+            ts(v("qq", off(m), off(m) + 16 * m), v(tr, 128, 128 + 16 * m), v("hold", 16 * m + 15, 16 * m + 16), A.not_equal)
+            next(steps, None)
         if t == 0:
             fill(v("base", 16, 17), -4.0)
             quant("f0", v("hin"), 128)
             quant("e", v("ctile"), 512)
             decode_x(0, range(4))
+        cp(v("nw16"), v("hold", 15, 256, 16))
+        for x in steps:
+            pass
+        if t > 0:
+            for b in range(4):
+                border_gather(t - 1, b, "S")
         scan(v("sc"), v("inc"), v("qq"), 4.0, A.add, A.min)
-        tt(v("t32"), ind(v("sc"), v("ends")), v("base"), A.subtract)
-        tt(v("w1"), v("t32", 0, 16), v("t32", 16, 32), A.min)
         if t > 0:
             border_send(t - 1)
+        tt(v("t32"), ind(v("sc"), v("ends")), v("base"), A.subtract)
+        if t > 0:
             names_in(t)
         tt(v("pl"), ind(v("pt%d" % t), v("nw16")), v("diag"), A.mult)
+        tt(v("w1"), v("t32", 0, 16), v("t32", 16, 32), A.min)
         scan(v("plh"), v("keep", 0, 256), v("pl"), 0.0, A.mult, A.add)
         tt(v("w"), v("w1"), v("plh", 15, 256, 16), A.min)
         ts(v("v16"), v("w"), -512.0, A.mult, 128.0, A.add)
@@ -384,38 +406,57 @@ def rank_program(g, core, T, topo):
         act(v("vr"), ind(v("iota"), v("v16")), F.Copy)
         act(v("e32", 0, 16), v("w"), F.Identity, bias=v("bm1"), scale=512.0)
         for m in range(MS, 16):
-            act(v("junk", 0, 16 * m), v("vr", 0, 16 * m), F.Sign, bias=v("vw", m, m + 1), scale=-1.0, acc=v("acc", m, m + 1))
+            act(junk(16 * m), v("vr", 0, 16 * m), F.Sign, bias=v("vw", m, m + 1), scale=-1.0, acc=v("acc", m, m + 1))
         act(v("e32", 16 + MS, 32), v("acc", MS, 16), F.Copy, scale=0.5)
         tt(v("vm"), ind(v("iota"), v("v16")), v("maskb"), A.add)
+
+        def shorter(a, b):
+            for m in range(a, b):
+                ts(v("lt", off(m), off(m) + 16 * m), v("vr", 0, 16 * m), v("vw", m, m + 1), A.is_lt)
+
+        shorter(1, 2)
         tt(v("lt", 0, 256), ind(v("vw"), v("lm")), v("vm"), A.is_gt)
-        for m in range(1, MS):
-            ts(v("lt", off(m), off(m) + 16 * m), v("vr", 0, 16 * m), v("vw", m, m + 1), A.is_lt)
-        scan(v("sc2", 0, S2), v("keep", 0, S2), v("lt"), 0.0, A.mult, A.add)
-        tt(v("dd"), ind(v("sc2"), v("ends2")), v("e32"), A.add)
-        tt(v("d"), v("dd", 0, 16), v("dd", 16, 32), A.add)
-        cp(v("d16"), v("d"))
+        shorter(2, 4)
+        scan(v("sc2", 0, 256), v("keep", 0, 256), v("lt", 0, 256), 0.0, A.mult, A.add)
+        shorter(4, MS)
+        tt(v("dd"), v("sc2", 15, 256, 16), v("e32", 0, 16), A.add)
+        scan(v("sc2", 256, S2), v("keep", 256, S2), v("lt", 256, S2), 0.0, A.mult, A.add)
+        tt(v("dd", MS, 16), v("dd", MS, 16), v("e32", 16 + MS, 32), A.add)
+        tt(v("d"), ind(v("sc2"), v("ends2")), v("dd"), A.add)
         if t == 0:
+            cp(v("d16"), v("d"))
             copy_x(0, (0, 1))
+        else:
+            ts(v("d16"), v("d"), -1.0, A.mult, 127.0, A.add)
         decode_f(t)
-        for b in (2, 3):
-            act(v("es", 256 * (b - 2), 256 * (b - 1)), ind(front_of(t, b), v("d16")), F.Copy)
+        for hf in (0, 1):
+            for b in (2, 3):
+                a = 256 * (b - 2) + 128 * hf
+                act(v("es", a, a + 128), ind(front_of(t, b), v("d16", 8 * hf, 8 * hf + 8)), F.Copy)
+        for hf in (0, 1):
+            a, e = 128 * hf, 128 * hf + 128
+            for b in (0, 1):
+                tt(v("zt", 4 * a + b, 4 * e, 4), ind(front_of(t, b), v("d16", 8 * hf, 8 * hf + 8)), x_of(t, b, a, e), A.add)
+            for b in (2, 3):
+                tt(v("zt", 4 * a + b, 4 * e, 4), v("es", 256 * (b - 2) + a, 256 * (b - 2) + e), ps(4 + b, 128, a), A.add)
+            quant("z", v("zt", 4 * a, 4 * e), 128, a)
+            for b in range(4):
+                mm(4 * hf + b, 128, "w", 128 * b, "z", a)
+        for hf in (0, 1):
+            a, e = 128 * hf, 128 * hf + 128
+            for b in range(4):
+                act(v("yt", 4 * a + b, 4 * e, 4), ps(4 * hf + b, 128), F.Copy, scale=0.03125)
+            quant("x%d" % (t + 1), v("yt", 4 * a, 4 * e), 128, a)
+            if t < R - 1:
+                mm(hf, 128, "u", 0, "x%d" % (t + 1), a)
+            if hf == 0:
+                border_alive(t)
         names_row(t)
-        for b in (0, 1):
-            tt(v("zt", b, 1024, 4), ind(front_of(t, b), v("d16")), v(gname(t), 384 * b, 384 * b + 256), A.add)
-        for b in (2, 3):
-            tt(v("zt", b, 1024, 4), v("es", 256 * (b - 2), 256 * (b - 1)), ps(4 + b, 256), A.add)
-        quant("z", v("zt"), 256)
-        for b, bank in enumerate((0, 2, 3, 4)):
-            mm(bank, 256, "w", 128 * b, "z")
-        border_list_1(t)
-        for b, bank in enumerate((0, 2, 3)):
-            act(v("yt", b, 1024, 4), ps(bank, 256), F.Copy, scale=0.03125)
-        ts(v("yt", 3, 1024, 4), ps(4, 256), 0.03125, A.mult)
-        quant("x%d" % (t + 1), v("yt"), 256)
-        border_list_2(t)
+        border_count(t)
 
     decode_x(R, range(4))
-    border_list_3(R - 1)
+    for x in border_list(R - 1):
+        pass
     copy_x(R, (0, 1))
     copy_x(R, (2, 3), "V")
     for b in (0, 1):
@@ -426,7 +467,7 @@ def rank_program(g, core, T, topo):
     quant("v", v("vin"), 128)
     mm(1, 256, "v", 0, "x3")
     act(v("ysb", 0, 256), ps(1, 256), F.Copy)
-    act(v("olb", 0, 256), ind(v("iotap"), v("d16")), F.Copy)
+    act(v("olb", 0, 256), ind(v("iotap"), v("d16")), F.Identity, bias=v("b127"), scale=-1.0)
 
     def stores(a, n, q, s):
         dma("Y", T.oc[:, 4 * a:4 * (a + n)], T[q][:, 0:n].bitcast(dt.uint8), v(q)[1], [])
@@ -447,6 +488,6 @@ def rank_program(g, core, T, topo):
     for i in range(dmas[0]):
         g.wait_ge(T.sem["d%d" % i], 16)
     for i in range(R):
-        g.wait_ge(T.sem["ra%d" % i], len(names_eng))
-        g.wait_ge(T.sem["rb%d" % i], 5)
+        g.wait_ge(T.sem["ra%d" % i], len(eng))
+        g.wait_ge(T.sem["rb%d" % i], 2 * len(eng))
     g.wait_ge(T.sem.left, left[0])

@@ -77,17 +77,17 @@ def rank_program(g, core, T, topo):
     def need_of(q, reads, writes):
         needs = {}
         for refs, wr in ((reads, False), (writes, True)):
-            for name, lo, hi in refs:
+            for name, lo, hi, *ph in refs:
                 psum = SCRATCH[name][0] == "psum"
-                for l, h, w, q2, s, n in hist.get(name, []):
-                    if l < hi and lo < h and (w or wr or (psum and q2 != q)):
+                for l, h, w, q2, s, n, *ph2 in hist.get(name, []):
+                    if l < hi and lo < h and (w or wr or (psum and q2 != q)) and not (ph and ph2 and ph != ph2):
                         needs[s] = max(needs.get(s, 0), n)
         return needs
 
     def note(q, reads, writes, s, n):
-        for name, lo, hi in writes:
-            hist[name] = [r for r in hist.get(name, []) if not (lo <= r[0] and r[1] <= hi)] + [(lo, hi, True, q, s, n)]
-        for name, lo, hi in reads:
+        for name, lo, hi, *ph in writes:
+            hist[name] = [r for r in hist.get(name, []) if not (lo <= r[0] and r[1] <= hi and (not ph or list(r[6:]) == ph))] + [(lo, hi, True, q, s, n, *ph)]
+        for name, lo, hi, *ph in reads:
             hist[name] = [r for r in hist.get(name, []) if r[2] or r[3] != q or not (lo <= r[0] and r[1] <= hi)] + [(lo, hi, False, q, s, n)]
 
     def emit(q, fn, reads, writes):
@@ -110,7 +110,7 @@ def rank_program(g, core, T, topo):
             return v("tiny", o + a, o + (n if b is None else b), st)
         b = SCRATCH[name][1][1] if b is None else b
         view = T[name][:, a:b] if st is None else T[name][:, a:b:st]
-        return view, [(name, a, b)]
+        return view, [(name, a, b) if st != 4 else (name, a, b, a % 4)]
 
     def ps(bank, n, a=0):
         return T["p%d" % bank][:, a:a + n], [("p%d" % bank, 0, 512)]
@@ -231,6 +231,8 @@ def rank_program(g, core, T, topo):
     act(v("keep", 1280, 2176), v("keep", 256, 1152), F.Copy)
     for m in range(1, 16):
         act(v("keep", off(m), off(m) + 1), v("diag", 0, 1), F.Copy, scale=0.0)
+    act(v("base"), v("base"), F.Copy, scale=1.0 / 512)
+    act(v("zeros"), v("diag"), F.Copy, scale=0.0)
 
     def x_of(t, b, a=0, e=256):
         return v("gx" if t == 0 else "g%d" % (t - 1), 384 * b + 128 + a, 384 * b + 128 + e)
@@ -362,11 +364,9 @@ def rank_program(g, core, T, topo):
         scan(v("hold"), v("keep", 0, 256), v("hm"), 0.0, A.mult, A.add)
         tt(v("qq", 0, 256), ind(v("hold"), v("lh")), v("nmask"), A.not_equal)
         if t == 0:
-            act(v("inc"), v("keep"), F.Identity, bias=v("b4"), scale=1.0 / 512 - 4.0)
-            act(v("base"), v("base"), F.Copy, scale=1.0 / 512)
             for b in range(4):
                 act(v("ctile", 512 * b + b, 512 * b + 512, 4), v("idn"), F.Copy)
-            act(v("zeros"), v("diag"), F.Copy, scale=0.0)
+            act(v("inc"), v("keep"), F.Identity, bias=v("b4"), scale=1.0 / 512 - 4.0)
             ts(v("plc"), v("iotap", 0, 128), 1.0 / 512, A.mult, 1.0 / 512, A.add)
             ts(v("plcr"), v("iotap", 0, 128), -1.0 / 512, A.mult, 128.0 / 512, A.add)
             cp(v("la0"), v("nmi"))
@@ -377,6 +377,7 @@ def rank_program(g, core, T, topo):
         if t > 0:
             copy_x(t, range(4))
         steps = border_list(t - 1) if t > 0 else iter(())
+        next(steps, None)
         for m in range(1, SQ):
             ts(v("qq", off(m), off(m) + 16 * m), v(tr, 128, 128 + 16 * m), v("hold", 16 * m + 15, 16 * m + 16), A.not_equal)
             next(steps, None)
@@ -414,9 +415,8 @@ def rank_program(g, core, T, topo):
             for m in range(a, b):
                 ts(v("lt", off(m), off(m) + 16 * m), v("vr", 0, 16 * m), v("vw", m, m + 1), A.is_lt)
 
-        shorter(1, 2)
         tt(v("lt", 0, 256), ind(v("vw"), v("lm")), v("vm"), A.is_gt)
-        shorter(2, 4)
+        shorter(1, 4)
         scan(v("sc2", 0, 256), v("keep", 0, 256), v("lt", 0, 256), 0.0, A.mult, A.add)
         shorter(4, MS)
         tt(v("dd"), v("sc2", 15, 256, 16), v("e32", 0, 16), A.add)
@@ -442,6 +442,8 @@ def rank_program(g, core, T, topo):
             quant("z", v("zt", 4 * a, 4 * e), 128, a)
             for b in range(4):
                 mm(4 * hf + b, 128, "w", 128 * b, "z", a)
+        border_alive(t)
+        names_row(t)
         for hf in (0, 1):
             a, e = 128 * hf, 128 * hf + 128
             for b in range(4):
@@ -449,9 +451,6 @@ def rank_program(g, core, T, topo):
             quant("x%d" % (t + 1), v("yt", 4 * a, 4 * e), 128, a)
             if t < R - 1:
                 mm(hf, 128, "u", 0, "x%d" % (t + 1), a)
-            if hf == 0:
-                border_alive(t)
-        names_row(t)
         border_count(t)
 
     decode_x(R, range(4))

@@ -2,16 +2,23 @@ from concourse.mybir import dt, AluOpType as A, ActivationFunctionType as F, Axi
 
 C, K, R = 256, 128, 3
 MS = 11
-SQ = 14
-NLAST = 5
+NMID = 7
+NEARLY = 5
+NLAST = 4
+LSTEP = 9
+YV = 3
 HALF = 0.5
 
 
-def off(m):
-    return 256 + 8 * m * (m - 1)
+def off1(m):
+    return 8 * m * (m + 1)
 
 
-S1, S2 = off(16), off(MS)
+def off2(m):
+    return 256 + 16 * MS * (m - 1) if 2 * m <= MS else 256 + 16 * MS * (MS - m - 1) + 16 * (MS - m)
+
+
+S2 = 256 + 8 * MS * (MS - 1)
 BF, F32, I32, U16, U8, Q8 = "bfloat16", "float32", "int32", "uint16", "uint8", "float8_e4m3fn_x4"
 SCRATCH, TINY = {}, {}
 
@@ -21,21 +28,23 @@ def buf(name, n, d=BF, where="sbuf"):
 
 
 for _n, _w in (("xin", 1024), ("hin", 512), ("uin", 512), ("vin", 512), ("bits", 512), ("ctile", 2048), ("ntile", 1024),
-               ("zt", 1024), ("yt", 1024), ("blk", 128), ("idn", 128), ("w56", 56), ("r16", 256), ("diag", 256), ("maskb", 256),
-               ("keep", 2176), ("inc", 2176), ("iota", 384), ("plc", 128), ("plcr", 128), ("zeros", 256), ("ones", 384), ("hm", 256),
-               ("hold", 256), ("nmask", 256), ("qq", 2176), ("sc", 2176), ("pl", 256), ("plh", 256), ("vr", 256), ("vm", 256), ("vw", 16),
-               ("lt", S2), ("sc2", S2 + 16), ("junk", 1536), ("ltb", 272), ("mn", 128), ("mh", 128), ("es", 512), ("arow", 384), ("gx", 1536)):
+               ("zt", 1024), ("yt", 1024), ("blk", 128), ("idn", 128), ("o16", 16), ("pe16", 16), ("r16", 256), ("diag", 256),
+               ("keep", 256), ("keep2", S2), ("tmpl", 272), ("own1", 16), ("own2", 16), ("inc", 2176), ("iota", 384), ("plc", 128),
+               ("plcr", 128), ("zeros", 256), ("ones", 384), ("hm", 256), ("hold", 256), ("qq", 2176), ("sc", 2176), ("pl", 256),
+               ("plh", 256), ("vr", 256), ("vw", 16), ("lt", S2), ("sc2", S2 + 16), ("junk", 1536), ("ltb", 816), ("cs", 2176),
+               ("mn", 128), ("mh", 128), ("arow", 384), ("gx", 1536)):
     buf(_n, _w)
-for _n, _w in (("kap", 1), ("pw", 1), ("k2", 1), ("e1", 1), ("e2", 1), ("pe", 1), ("sel1", 1), ("sel2", 1), ("pr", 1), ("base", 32), ("thr", 8),
-               ("thr0", 8), ("thrl", 8), ("t32", 32), ("w1", 16), ("w", 16), ("acc", 16), ("e32", 32), ("dd", 16), ("d", 16), ("accb", 8), ("ct", 8),
-               ("sa_", 8), ("sb_", 8), ("sc_", 8), ("sf_", 8), ("b1", 1), ("b4", 1), ("c2", 8), ("c2l", 8), ("b127", 1), ("bm1", 1)):
+for _n, _w in (("kap", 1), ("pw", 1), ("k1", 1), ("k2", 1), ("e1", 1), ("e2", 1), ("e3", 1), ("pe", 1), ("sel1", 1), ("sel2", 1), ("pr", 1),
+               ("base", 16), ("base0", 16), ("thr", 8), ("pwv", 16),
+               ("thr0", 8), ("thrl", 8), ("x1", 16), ("nh", 16), ("w1", 16), ("w", 16), ("acc", 16), ("e32", 32), ("dd", 16), ("d", 16), ("accb", 8),
+               ("sa_", 8), ("sb_", 8), ("sc_", 8), ("sf_", 8), ("c2", 8), ("c2l", 8), ("b127", 1), ("bm64", 1)):
     TINY[_n] = (sum(w for o, w in TINY.values()), _w)
 buf("tiny", sum(w for o, w in TINY.values()), F32)
 for _n, _w in (("ysb", 384), ("olb", 384), ("iotap", 256)):
     buf(_n, _w, F32)
-for _n, _w in (("qi", 1), ("qi2", 1), ("il", 16), ("im", 16), ("nmi", 8)):
+for _n, _w in (("qi", 1), ("qi2", 1), ("im", 16), ("nmi", 8)):
     buf(_n, _w, I32)
-for _n, _w in (("lh", 16), ("lm", 16), ("ends", 2), ("ends2", 1), ("nw16", 16), ("v16", 16), ("d16", 16), ("src16", 8), ("la0", 8)):
+for _n, _w in (("lm", 16), ("ends", 1), ("ends2", 1), ("nw16", 16), ("v16", 16), ("d16", 16), ("src16", 8), ("la0", 8)):
     buf(_n, _w, U16)
 for _t in range(R):
     buf("g%d" % _t, 1536)
@@ -66,7 +75,7 @@ def rank_program(g, core, T, topo):
     semof = {"V": "cv", "S": "cs", "P": "cp", "G": "cg"}
     count = {"cv": 0, "cs": 0, "cp": 0, "cg": 0}
     seen = {q: {} for q in queues}
-    hist, dmas, left, turn = {}, [0], [0], [0]
+    hist, dmas, left, turn = {}, [0], [0], [0, 0]
 
     def wait(q, needs):
         for s in sorted(needs):
@@ -138,9 +147,6 @@ def rank_program(g, core, T, topo):
     def scan(o, d0, d1, init, op0, op1):
         emit("V", lambda: g.vector.tensor_tensor_scan(o[0], d0[0], d1[0], init, op0, op1), d0[1] + d1[1], o[1])
 
-    def total(o, a):
-        emit("V", lambda: g.vector.tensor_reduce(o[0], a[0], AxisListType.X, A.add), a[1], o[1])
-
     def fill(o, c):
         emit("V", lambda: g.vector.memset(o[0], c), [], o[1])
 
@@ -182,57 +188,55 @@ def rank_program(g, core, T, topo):
     dma("Y", T.vin[:], T.v[:], [], v("vin")[1])
 
     iota(v("qi"), [[0, 1]], 0, 1, small=False)
-    fill(v("w56"), 0.0)
+    iota(v("o16"), [[1, 16]])
     fill(v("blk"), 1.0)
-    for i in range(7):
-        fill(v("w56", i, 56, 7), float(2 ** i))
-    fill(v("idn"), HALF)
+    fill(v("tmpl", 0, 240), 1.0)
+    fill(v("tmpl", 256, 257), 2048.0)
     keep_where(v("blk"), [[-16, 8], [0, 16]], A.is_ge, 0, 1)
     keep_where(v("blk"), [[16, 8], [0, 16]], A.is_ge, 15, -1)
-    keep_where(v("w56"), [[-16, 8], [-1, 7]], A.is_equal, 0, 1)
     iota(v("r16"), [[0, 16], [1, 16]])
-    keep_where(v("idn"), [[-1, 128]], A.is_equal, 0, 1)
-    iota(v("il"), [[16, 16]], 15, 0, small=False)
+    emit("V", lambda: g.vector.tensor_scalar(T.qi2[:], T.qi[:], 15, None, A.bitwise_and), v("qi")[1], v("qi2")[1])
+    cp(v("kap"), v("qi2"))
+    fill(v("inc", 0, 1), 2048.0)
+    ts(v("own1"), v("o16"), v("kap"), A.is_lt)
+    ts(v("own2"), v("o16"), v("kap"), A.is_equal, -256.0, A.mult)
+    ts(v("pe16"), v("o16"), v("kap"), A.is_lt, 1.0, A.add)
+    tt(v("tmpl", 240, 256), v("own1"), v("own2"), A.add)
+    scan(v("pwv"), v("pe16"), v("pe16"), 1.0, A.mult, A.max)
+    fill(v("ntile"), 0.0)
+    for m in range(15, -1, -1):
+        n = 16 * m + 15 + (m < 15)
+        act(v("inc", off1(m) + 1, off1(m) + 1 + n), v("tmpl", 241 - 16 * m, 241 - 16 * m + n), F.Copy)
+    ts(v("pw"), v("kap"), 6.5, A.is_lt, v("pwv", 15, 16), A.mult)
+    fill(v("bits"), 0.0)
     iota(v("im"), [[1, 16]], 0, 0, small=False)
-    iota(v("iotap"), [[1, 256]])
-    iota(v("base"), [[-16, 2], [16, 16]], 15)
+    iota(v("base0"), [[16, 16]], -257)
+    iota(v("plc"), [[1, 128]], 1)
+    iota(v("plcr"), [[-1, 128]], 128)
+    fill(v("idn"), HALF)
+    keep_where(v("idn"), [[-1, 128]], A.is_equal, 0, 1)
+    iota(v("ctile"), [[0, 2048]])
     iota(v("iota"), [[1, 384]], -128)
-    iota(v("sc2", S2, S2 + 16), [[8, 16]])
+    iota(v("iotap"), [[1, 256]])
+    iota(v("keep2", 256, S2), [[0, S2 - 256]], 1)
+    iota(v("sc2", S2, S2 + 16), [[512, 16]])
+    iota(v("zeros"), [[0, 256]])
+    iota(v("alive0"), [[0, 384]], 1)
+    iota(v("ones"), [[0, 384]], 1)
     iota(v("thr0"), [[16, 8]])
     iota(v("c2"), [[32, 8]], 272)
     iota(v("c2l"), [[-32, 8]], 496)
-    fill(v("ntile"), 0.0)
-    fill(v("bits"), 0.0)
-    fill(v("b1"), 1.0)
-    emit("V", lambda: g.vector.tensor_scalar(T.qi2[:], T.qi[:], 15, None, A.bitwise_and), v("qi")[1], v("qi2")[1])
-    cp(v("kap"), v("qi2"))
-    total(v("pw"), v("w56"))
+    for i in range(1, R):
+        iota(v("alive%d" % i), [[0, 384]], 1)
     ts(v("ntile", 0, 512, 4), v("blk"), v("pw"), A.mult)
     ts(v("ntile", 513, 1024, 4), v("blk"), v("pw"), A.mult)
     quant("n", v("ntile"), 256)
-    ts(v("diag"), v("r16"), v("kap"), A.is_equal)
-    ts(v("maskb"), v("r16"), v("kap"), A.is_ge, 512.0, A.mult)
-    ts(v("keep", 0, 256), v("r16"), 0.0, A.not_equal)
     quant("u", v("uin"), 128)
-    tt(v("k2"), v("kap"), v("kap"), A.mult)
-    ts(v("e1"), v("k2"), 8.0, A.mult, 255.0, A.add)
-    ts(v("pe"), v("kap"), 8.0, A.mult, v("e1"), A.add)
-    ts(v("e2"), v("kap"), float(S2), A.add)
-    ts(v("sel1"), v("kap"), 0.5, A.is_ge)
-    ts(v("sel2"), v("kap"), MS - 0.5, A.is_lt, v("sel1"), A.mult)
-    ts(v("pr"), v("pe"), v("e2"), A.subtract, v("sel2"), A.mult)
-    ts(v("ends", 0, 1), v("kap"), 16.0, A.mult, 15.0, A.add)
-    cp(v("ends", 1, 2), v("pe"))
-    ts(v("ends2"), v("pr"), v("e2"), A.add)
-    quant("x0", v("xin"), 256)
-    act(v("keep", 256, 512), v("diag"), F.Identity, bias=v("b1"), scale=0.0)
-    act(v("keep", 512, 768), v("keep", 256, 512), F.Copy)
-    act(v("keep", 768, 1280), v("keep", 256, 768), F.Copy)
-    act(v("keep", 1280, 2176), v("keep", 256, 1152), F.Copy)
-    for m in range(1, 16):
-        act(v("keep", off(m), off(m) + 1), v("diag", 0, 1), F.Copy, scale=0.0)
-    act(v("base"), v("base"), F.Copy, scale=1.0 / 512)
-    act(v("zeros"), v("diag"), F.Copy, scale=0.0)
+    ts(v("diag"), v("r16"), v("kap"), A.is_equal)
+    for hf in (0, 1):
+        quant("x0", v("xin", 512 * hf, 512 * hf + 512), 128, 128 * hf)
+        mm(hf, 128, "u", 0, "x0", 128 * hf)
+    ts(v("keep"), v("r16"), 0.0, A.not_equal)
 
     def x_of(t, b, a=0, e=256):
         return v("gx" if t == 0 else "g%d" % (t - 1), 384 * b + 128 + a, 384 * b + 128 + e)
@@ -286,12 +290,6 @@ def rank_program(g, core, T, topo):
             hist[n % (t + 1)] = [(0, 128, True, "R", "rb%d" % t, 2 * len(eng))]
 
     def border_alive(t):
-        if t == 0:
-            ts(v("thr"), v("thr0"), v("kap"), A.add, 0.5, A.add)
-            ts(v("thrl"), v("thr"), -1.0, A.mult, 128.0, A.add)
-            fill(v("ones"), 1.0)
-            for i in range(R):
-                fill(v("alive%d" % i), 1.0)
         emit("V", lambda: g.vector.tensor_copy(T["alive%d" % t][:, 0:384].indirect(T.v16[:, 0:16]), T.zeros[:]),
              v("zeros")[1] + v("v16")[1] + v("alive%d" % t)[1], v("alive%d" % t)[1])
         scan(v("arow"), v("ones"), v("alive%d" % t), 0.0, A.mult, A.add)
@@ -300,21 +298,23 @@ def rank_program(g, core, T, topo):
         turn[0] = (turn[0] + 1) % 4
         return v("junk", 384 * turn[0], 384 * turn[0] + n)
 
-    def border_count(t):
+    def border_count(t, ms, q="S"):
         last = t == R - 1
-        n, thr = (NLAST, "thrl") if last else (8, "thr")
-        for m in range(8):
+        thr = "thrl" if last else "thr"
+        for m in ms:
             a = 112 - 16 * m if last else 16 * m
-            if m < n:
+            if q == "S":
                 act(junk(272), v("arow", a, a + 272), F.Sign, bias=v(thr, m, m + 1), scale=-1.0, acc=v("accb", m, m + 1))
             else:
-                ts(v("ltb"), v("arow", a, a + 272), v(thr, m, m + 1), A.is_lt, 2.0, A.mult)
-                total(v("ct", m, m + 1), v("ltb"))
-        if n < 8:
-            ts(v("accb", n, 8), v("ct", n, 8), -272.0, A.add)
+                turn[1] = (turn[1] + 1) % 3
+                o = v("ltb", 272 * turn[1], 272 * turn[1] + 272)
+                ts(o, v("arow", a, a + 272), v(thr, m, m + 1), A.is_lt, 2.0, A.mult)
+                scan(v("cs", 272 * m, 272 * m + 272), v("ones", 0, 272), o, -272.0, A.mult, A.add)
 
-    def border_list(t):
-        yield tt(v("sb_"), v("accb"), v("c2l" if t == R - 1 else "c2"), A.add)
+    def border_columns(t):
+        n, c2 = (NLAST, "c2l") if t == R - 1 else (NMID, "c2")
+        yield tt(v("sb_", n, 8), v("cs", 272 * n + 271, 2176, 272), v(c2, n, 8), A.add)
+        yield tt(v("sb_", 0, n), v("accb", 0, n), v(c2, 0, n), A.add)
         if t == 0:
             yield ts(v("sa_"), v("sb_"), 255.5, A.is_ge, 0.5, A.mult)
             yield ts(v("sc_"), v("sb_"), -0.5, A.mult, 127.0, A.add)
@@ -323,11 +323,16 @@ def rank_program(g, core, T, topo):
             yield cp(v("src16"), v("sf_"))
         else:
             yield ts(v("src16"), v("sb_"), 0.5, A.mult)
+
+    def border_names(t):
         yield tt(v("mn"), ind(v("trw%d" % t), v("src16")), v("diag", 0, 128), A.mult)
         yield scan(v("mh"), v("keep", 0, 128), v("mn"), 0.0, A.mult, A.add)
         yield cp(v("sa%d" % t), v("mh", 15, 128, 16))
         send_names(t)
-        yield None
+
+    def border_list(t):
+        yield from border_columns(t)
+        yield from border_names(t)
 
     def border_gather(t, b, q):
         o, i = v("bt%d" % t, b, 512, 4), ind(v("g%d" % t, 384 * b, 384 * b + 384), v("src16"))
@@ -336,133 +341,145 @@ def rank_program(g, core, T, topo):
         else:
             ts(o, i, 2.0, A.mult)
 
-    mm(0, 128, "u", 0, "x0", 0)
-    mm(1, 128, "u", 0, "x0", 128)
     for t in range(R):
         tr = "trw%d" % t
-        if t == 0:
-            fill(v("b4"), 4.0)
-            fill(v("bm1"), -1.0)
-            fill(v("b127"), 127.0)
-            cp(v("lh"), v("il"))
         ts(v("bits", 0, 512, 4), ps(0, 128), 0.0, A.is_lt)
         ts(v("bits", 1, 512, 4), ps(1, 128), 0.0, A.is_lt)
         quant("bit", v("bits"), 128)
-        if t > 0:
-            decode_x(t, (0, 1))
         mm(2, 128, "n", 0, "bit")
         mm(3, 128, "n", 128, "bit")
-        if t == 0:
-            fill(v("ctile"), 0.0)
+        if t > 0:
+            decode_x(t, range(4))
+            border_count(t - 1, range(NMID, 8), "V")
         else:
-            decode_x(t, (2, 3))
-        for hf in (0, 1):
-            a, e = 128 * hf, 128 * hf + 128
-            tt(v("hm", a, e), ps(2 + hf, 128), v("diag", a, e), A.mult)
-            tt(v("nmask", a, e), ps(2 + hf, 128), v("maskb", a, e), A.add)
-            act(v(tr, 128 + a, 128 + e), ps(2 + hf, 128), F.Copy)
-        scan(v("hold"), v("keep", 0, 256), v("hm"), 0.0, A.mult, A.add)
-        tt(v("qq", 0, 256), ind(v("hold"), v("lh")), v("nmask"), A.not_equal)
-        if t == 0:
-            for b in range(4):
-                act(v("ctile", 512 * b + b, 512 * b + 512, 4), v("idn"), F.Copy)
-            act(v("inc"), v("keep"), F.Identity, bias=v("b4"), scale=1.0 / 512 - 4.0)
-            ts(v("plc"), v("iotap", 0, 128), 1.0 / 512, A.mult, 1.0 / 512, A.add)
-            ts(v("plcr"), v("iotap", 0, 128), -1.0 / 512, A.mult, 128.0 / 512, A.add)
             cp(v("la0"), v("nmi"))
             names_in(0)
             cp(v("lm"), v("im"))
-        for m in range(SQ, 16):
-            act(v("qq", off(m), off(m) + 16 * m), v(tr, 128, 128 + 16 * m), F.Square, bias=v("hold", 16 * m + 15, 16 * m + 16), scale=-1.0)
+        for hf in (0, 1):
+            a, e = 128 * hf, 128 * hf + 128
+            tt(v("hm", a, e), ps(2 + hf, 128), v("diag", a, e), A.mult)
+            act(v(tr, 128 + a, 128 + e), ps(2 + hf, 128), F.Copy)
         if t > 0:
+            border_count(t - 1, range(NEARLY, NMID))
+        scan(v("hold"), v("keep"), v("hm"), 0.0, A.mult, A.add)
+        if t == 0:
+            for b in range(4):
+                act(v("ctile", 512 * b + b, 512 * b + 512, 4), v("idn"), F.Copy)
+            ts(v("base"), v("base0"), v("kap"), A.add)
+            ts(v("k1"), v("kap"), 1.5, A.add)
+            ts(v("e1"), v("kap"), 16.0 * MS + 16.0, A.mult, 255.0 - 16.0 * MS, A.add)
+            ts(v("e3"), v("kap"), -16.0 * MS, A.mult, 255.0 + 16.0 * MS * MS, A.add)
+            ts(v("e2"), v("kap"), float(S2), A.add)
+            ts(v("sel1"), v("kap"), 0.5, A.is_ge)
+            tt(v("k2"), v("k1"), v("k1"), A.mult)
+            tt(v("pe"), v("e1"), v("e3"), A.min)
+            ts(v("sel2"), v("kap"), MS - 0.5, A.is_lt, v("sel1"), A.mult)
+            ts(v("ends"), v("k2"), 8.0, A.mult, -3.0, A.add)
+            ts(v("pr"), v("pe"), v("e2"), A.subtract, v("sel2"), A.mult)
+            fill(v("bm64"), -64.0)
+            ts(v("ends2"), v("pr"), v("e2"), A.add)
+        else:
             copy_x(t, range(4))
         steps = border_list(t - 1) if t > 0 else iter(())
-        next(steps, None)
-        for m in range(1, SQ):
-            ts(v("qq", off(m), off(m) + 16 * m), v(tr, 128, 128 + 16 * m), v("hold", 16 * m + 15, 16 * m + 16), A.not_equal)
-            next(steps, None)
-        if t == 0:
-            fill(v("base", 16, 17), -4.0)
-            quant("f0", v("hin"), 128)
-            quant("e", v("ctile"), 512)
-            decode_x(0, range(4))
+        for m in range(16):
+            ts(v("qq", off1(m), off1(m + 1)), v(tr, 128, 144 + 16 * m), v("hold", 16 * m + 15, 16 * m + 16), A.not_equal, 1024.0, A.mult)
+            if m >= LSTEP:
+                next(steps, None)
         cp(v("nw16"), v("hold", 15, 256, 16))
         for x in steps:
             pass
-        if t > 0:
+        if t == 0:
+            quant("f0", v("hin"), 128)
+        else:
             for b in range(4):
                 border_gather(t - 1, b, "S")
-        scan(v("sc"), v("inc"), v("qq"), 4.0, A.add, A.min)
+        scan(v("sc"), v("inc"), v("qq"), 0.0, A.add, A.min)
         if t > 0:
             border_send(t - 1)
-        tt(v("t32"), ind(v("sc"), v("ends")), v("base"), A.subtract)
+        else:
+            quant("e", v("ctile"), 512)
+            decode_x(0, range(4))
+            copy_x(0, range(4))
+        ts(v("nh"), ind(v("sc"), v("ends")), -0.5, A.is_ge, 1024.0, A.mult)
+        tt(v("x1"), ind(v("sc"), v("ends")), v("base"), A.subtract)
         if t > 0:
             names_in(t)
+        names_row(t)
         tt(v("pl"), ind(v("pt%d" % t), v("nw16")), v("diag"), A.mult)
-        tt(v("w1"), v("t32", 0, 16), v("t32", 16, 32), A.min)
-        scan(v("plh"), v("keep", 0, 256), v("pl"), 0.0, A.mult, A.add)
+        tt(v("w1"), v("x1"), v("nh"), A.add)
+        scan(v("plh"), v("keep"), v("pl"), 0.0, A.mult, A.add)
         tt(v("w"), v("w1"), v("plh", 15, 256, 16), A.min)
-        ts(v("v16"), v("w"), -512.0, A.mult, 128.0, A.add)
-        act(v("vw"), v("w"), F.Copy, scale=-512.0)
-        act(v("vr"), ind(v("iota"), v("v16")), F.Copy)
-        act(v("e32", 0, 16), v("w"), F.Identity, bias=v("bm1"), scale=512.0)
+        ts(v("v16"), v("w"), -1.0, A.mult, 128.0, A.add)
+        act(v("vw"), v("w"), F.Copy, scale=-1.0)
+        act(v("e32", 0, 16), v("w"), F.Identity, bias=v("bm64"), scale=64.0)
+        cp(v("vr"), ind(v("iota"), v("v16")))
+        if t == 0:
+            ts(v("keep2", 0, 256), v("diag"), 63.0, A.mult, 1.0, A.add)
+            fill(v("keep2", 0, 256, 16), 0.0)
+            fill(v("keep2", 256, S2, 16 * MS), 0.0)
+            fill(v("keep2", 272, S2, 16 * MS + 16), 0.0)
         for m in range(MS, 16):
             act(junk(16 * m), v("vr", 0, 16 * m), F.Sign, bias=v("vw", m, m + 1), scale=-1.0, acc=v("acc", m, m + 1))
-        act(v("e32", 16 + MS, 32), v("acc", MS, 16), F.Copy, scale=0.5)
-        tt(v("vm"), ind(v("iota"), v("v16")), v("maskb"), A.add)
+        act(v("e32", 16 + MS, 32), v("acc", MS, 16), F.Copy, scale=32.0)
 
         def shorter(a, b):
             for m in range(a, b):
-                ts(v("lt", off(m), off(m) + 16 * m), v("vr", 0, 16 * m), v("vw", m, m + 1), A.is_lt)
+                ts(v("lt", off2(m), off2(m) + 16 * m), v("vr", 0, 16 * m), v("vw", m, m + 1), A.is_lt, 64.0, A.mult)
 
-        tt(v("lt", 0, 256), ind(v("vw"), v("lm")), v("vm"), A.is_gt)
+        tt(v("lt", 0, 256), ind(v("vw"), v("lm")), v("vr"), A.is_gt)
         shorter(1, 4)
-        scan(v("sc2", 0, 256), v("keep", 0, 256), v("lt", 0, 256), 0.0, A.mult, A.add)
+        scan(v("sc2", 0, 256), v("keep2", 0, 256), v("lt", 0, 256), 0.0, A.mult, A.add)
         shorter(4, MS)
         tt(v("dd"), v("sc2", 15, 256, 16), v("e32", 0, 16), A.add)
-        scan(v("sc2", 256, S2), v("keep", 256, S2), v("lt", 256, S2), 0.0, A.mult, A.add)
+        scan(v("sc2", 256, S2), v("keep2", 256, S2), v("lt", 256, S2), 0.0, A.mult, A.add)
         tt(v("dd", MS, 16), v("dd", MS, 16), v("e32", 16 + MS, 32), A.add)
         tt(v("d"), ind(v("sc2"), v("ends2")), v("dd"), A.add)
         if t == 0:
-            cp(v("d16"), v("d"))
-            copy_x(0, (0, 1))
+            ts(v("d16"), v("d"), 1.0 / 64, A.mult)
         else:
-            ts(v("d16"), v("d"), -1.0, A.mult, 127.0, A.add)
+            ts(v("d16"), v("d"), -1.0 / 64, A.mult, 127.0, A.add)
         decode_f(t)
         for hf in (0, 1):
-            for b in (2, 3):
-                a = 256 * (b - 2) + 128 * hf
-                act(v("es", a, a + 128), ind(front_of(t, b), v("d16", 8 * hf, 8 * hf + 8)), F.Copy)
-        for hf in (0, 1):
             a, e = 128 * hf, 128 * hf + 128
-            for b in (0, 1):
+            for b in range(4):
                 tt(v("zt", 4 * a + b, 4 * e, 4), ind(front_of(t, b), v("d16", 8 * hf, 8 * hf + 8)), x_of(t, b, a, e), A.add)
-            for b in (2, 3):
-                tt(v("zt", 4 * a + b, 4 * e, 4), v("es", 256 * (b - 2) + a, 256 * (b - 2) + e), ps(4 + b, 128, a), A.add)
             quant("z", v("zt", 4 * a, 4 * e), 128, a)
             for b in range(4):
                 mm(4 * hf + b, 128, "w", 128 * b, "z", a)
+        if t == 0:
+            ts(v("thr"), v("thr0"), v("kap"), A.add, 0.5, A.add)
         border_alive(t)
-        names_row(t)
+        if t == 0:
+            ts(v("thrl"), v("thr"), -1.0, A.mult, 128.0, A.add)
+            fill(v("b127"), 127.0)
         for hf in (0, 1):
             a, e = 128 * hf, 128 * hf + 128
             for b in range(4):
-                act(v("yt", 4 * a + b, 4 * e, 4), ps(4 * hf + b, 128), F.Copy, scale=0.03125)
+                if hf == 1 and b >= YV:
+                    ts(v("yt", 4 * a + b, 4 * e, 4), ps(4 * hf + b, 128), 0.03125, A.mult)
+                else:
+                    act(v("yt", 4 * a + b, 4 * e, 4), ps(4 * hf + b, 128), F.Copy, scale=0.03125)
             quant("x%d" % (t + 1), v("yt", 4 * a, 4 * e), 128, a)
             if t < R - 1:
                 mm(hf, 128, "u", 0, "x%d" % (t + 1), a)
-        border_count(t)
+        if t < R - 1:
+            border_count(t, range(NEARLY))
 
     decode_x(R, range(4))
-    for x in border_list(R - 1):
+    border_count(R - 1, range(NLAST))
+    border_count(R - 1, range(NLAST, 7), "V")
+    copy_x(R, (0, 1, 3))
+    copy_x(R, (2,), "V")
+    border_count(R - 1, (7,), "V")
+    for x in border_columns(R - 1):
         pass
-    copy_x(R, (0, 1))
-    copy_x(R, (2, 3), "V")
     for b in (0, 1):
         border_gather(R - 1, b, "S")
     for b in (2, 3):
         border_gather(R - 1, b, "V")
     border_send(R - 1)
+    for x in border_names(R - 1):
+        pass
     quant("v", v("vin"), 128)
     mm(1, 256, "v", 0, "x3")
     act(v("ysb", 0, 256), ps(1, 256), F.Copy)
@@ -475,12 +492,12 @@ def rank_program(g, core, T, topo):
 
     dma("S", T.y[:, 0:256], T.ysb[:, 0:256], v("ysb", 0, 256)[1], [])
     stores(0, 256, "qx3", "sx3")
-    act(v("olb", 256, 384), ind(v("iotap"), v("la3")), F.Copy)
-    dma("Y", T.ol[:, :], T.olb[0:128:16, :], v("olb")[1], [])
     mm(2, 128, "v", 0, "f3")
     cp(v("ysb", 256, 384), ps(2, 128))
     stores(256, 128, "qf3", "sf3")
-    dma("S", T.y[:, 256:384], T.ysb[:, 256:384], v("ysb", 256, 384)[1], [])
+    dma("Y", T.y[:, 256:384], T.ysb[:, 256:384], v("ysb", 256, 384)[1], [])
+    act(v("olb", 256, 384), ind(v("iotap"), v("la3")), F.Copy)
+    dma("S", T.ol[:, :], T.olb[0:128:16, :], v("olb")[1], [])
 
     for s in ("cv", "cs", "cp", "cg"):
         g.wait_ge(T.sem[s], count[s])

from concourse.mybir import dt, AluOpType as A, ActivationFunctionType as F, AxisListType

C, K, R = 256, 128, 3
MS = 11
NMID = 7
NEARLY = 5
NLAST = 4
LSTEP = 9
YV = 3
HALF = 0.5


def off1(m):
    return 8 * m * (m + 1)


def off2(m):
    return 256 + 16 * MS * (m - 1) if 2 * m <= MS else 256 + 16 * MS * (MS - m - 1) + 16 * (MS - m)


S2 = 256 + 8 * MS * (MS - 1)
BF, F32, I32, U16, U8, Q8 = "bfloat16", "float32", "int32", "uint16", "uint8", "float8_e4m3fn_x4"
SCRATCH, TINY = {}, {}


def buf(name, n, d=BF, where="sbuf"):
    SCRATCH[name] = (where, [128, n], d)


for _n, _w in (("xin", 1024), ("hin", 512), ("uin", 512), ("vin", 512), ("bits", 512), ("ctile", 2048), ("ntile", 1024),
               ("zt", 1024), ("yt", 1024), ("blk", 128), ("idn", 128), ("o16", 16), ("pe16", 16), ("r16", 256), ("diag", 256),
               ("keep", 256), ("keep2", S2), ("tmpl", 272), ("own1", 16), ("own2", 16), ("inc", 2176), ("iota", 384), ("plc", 128),
               ("plcr", 128), ("zeros", 256), ("ones", 384), ("hm", 256), ("hold", 256), ("qq", 2176), ("sc", 2176), ("pl", 256),
               ("plh", 256), ("vr", 256), ("vw", 16), ("lt", S2), ("sc2", S2 + 16), ("junk", 1536), ("ltb", 816), ("cs", 2176),
               ("mn", 128), ("mh", 128), ("arow", 384), ("gx", 1536)):
    buf(_n, _w)
for _n, _w in (("kap", 1), ("pw", 1), ("k1", 1), ("k2", 1), ("e1", 1), ("e2", 1), ("e3", 1), ("pe", 1), ("sel1", 1), ("sel2", 1), ("pr", 1),
               ("base", 16), ("base0", 16), ("thr", 8), ("pwv", 16),
               ("thr0", 8), ("thrl", 8), ("x1", 16), ("nh", 16), ("w1", 16), ("w", 16), ("acc", 16), ("e32", 32), ("dd", 16), ("d", 16), ("accb", 8),
               ("sa_", 8), ("sb_", 8), ("sc_", 8), ("sf_", 8), ("c2", 8), ("c2l", 8), ("b127", 1), ("bm64", 1)):
    TINY[_n] = (sum(w for o, w in TINY.values()), _w)
buf("tiny", sum(w for o, w in TINY.values()), F32)
for _n, _w in (("ysb", 384), ("olb", 384), ("iotap", 256)):
    buf(_n, _w, F32)
for _n, _w in (("qi", 1), ("qi2", 1), ("im", 16), ("nmi", 8)):
    buf(_n, _w, I32)
for _n, _w in (("lm", 16), ("ends", 1), ("ends2", 1), ("nw16", 16), ("v16", 16), ("d16", 16), ("src16", 8), ("la0", 8)):
    buf(_n, _w, U16)
for _t in range(R):
    buf("g%d" % _t, 1536)
    buf("trw%d" % _t, 384)
    buf("pt%d" % _t, 128)
    buf("alive%d" % _t, 384)
    buf("bt%d" % _t, 512)
    buf("sa%d" % _t, 8, U16)
    buf("la%d" % (_t + 1), 8, U16)
    buf("qb%d" % _t, 128, Q8)
    buf("sb%d" % _t, 128, U8)
for _n, _w in (("u", 128), ("v", 128), ("w", 512), ("e", 512), ("n", 256), ("bit", 128), ("z", 256),
               ("x0", 256), ("x1", 256), ("x2", 256), ("x3", 256), ("f0", 128), ("f1", 128), ("f2", 128), ("f3", 128)):
    buf("q" + _n, _w, Q8)
    buf("s" + _n, _w, U8)
for _n in range(8):
    buf("p%d" % _n, 512, F32, "psum")

NDMA = 22
SEMAPHORES = ["cv", "cs", "cp", "cg", "left"] + ["ra%d" % t for t in range(R)] + ["rb%d" % t for t in range(R)] + ["d%d" % i for i in range(NDMA)]


def rank_program(g, core, T, topo):
    rank = T.rank_of(core)
    if rank is None:
        return
    queues = {"V": g.vector, "S": g.scalar, "P": g.tensor, "G": g, "Y": g.sync}
    semof = {"V": "cv", "S": "cs", "P": "cp", "G": "cg"}
    count = {"cv": 0, "cs": 0, "cp": 0, "cg": 0}
    seen = {q: {} for q in queues}
    hist, dmas, left, turn = {}, [0], [0], [0, 0]

    def wait(q, needs):
        for s in sorted(needs):
            if seen[q].get(s, 0) < needs[s]:
                queues[q].wait_ge(T.sem[s], needs[s])
                seen[q][s] = needs[s]

    def need_of(q, reads, writes):
        needs = {}
        for refs, wr in ((reads, False), (writes, True)):
            for name, lo, hi, *ph in refs:
                psum = SCRATCH[name][0] == "psum"
                for l, h, w, q2, s, n, *ph2 in hist.get(name, []):
                    if l < hi and lo < h and (w or wr or (psum and q2 != q)) and not (ph and ph2 and ph != ph2):
                        needs[s] = max(needs.get(s, 0), n)
        return needs

    def note(q, reads, writes, s, n):
        for name, lo, hi, *ph in writes:
            hist[name] = [r for r in hist.get(name, []) if not (lo <= r[0] and r[1] <= hi and (not ph or list(r[6:]) == ph))] + [(lo, hi, True, q, s, n, *ph)]
        for name, lo, hi, *ph in reads:
            hist[name] = [r for r in hist.get(name, []) if r[2] or r[3] != q or not (lo <= r[0] and r[1] <= hi)] + [(lo, hi, False, q, s, n)]

    def emit(q, fn, reads, writes):
        wait(q, need_of(q, reads, writes))
        s = semof[q]
        count[s] += 1
        fn().then_inc(T.sem[s], 1)
        note(q, reads, writes, s, count[s])

    def dma(q, o, i, reads, writes):
        wait(q, need_of(q, reads, writes))
        s = "d%d" % dmas[0]
        dmas[0] += 1
        queues[q].dma_start(o, i).then_inc(T.sem[s], 16)
        note(q + "d", reads, writes, s, 16)

    def v(name, a=0, b=None, st=None):
        if name in TINY:
            o, n = TINY[name]
            return v("tiny", o + a, o + (n if b is None else b), st)
        b = SCRATCH[name][1][1] if b is None else b
        view = T[name][:, a:b] if st is None else T[name][:, a:b:st]
        return view, [(name, a, b) if st != 4 else (name, a, b, a % 4)]

    def ps(bank, n, a=0):
        return T["p%d" % bank][:, a:a + n], [("p%d" % bank, 0, 512)]

    def ind(win, lst):
        return win[0].indirect(lst[0]), win[1] + lst[1]

    def tt(o, a, b, op):
        emit("V", lambda: g.vector.tensor_tensor(o[0], a[0], b[0], op), a[1] + b[1], o[1])

    def ts(o, a, s1, op0, s2=None, op1=None):
        r, x = list(a[1]), [s1, s2]
        for i in (0, 1):
            if isinstance(x[i], tuple):
                r += x[i][1]
                x[i] = x[i][0]
        if op1 is None:
            emit("V", lambda: g.vector.tensor_scalar(o[0], a[0], x[0], None, op0), r, o[1])
        else:
            emit("V", lambda: g.vector.tensor_scalar(o[0], a[0], x[0], x[1], op0, op1), r, o[1])

    def cp(o, a):
        emit("V", lambda: g.vector.tensor_copy(o[0], a[0]), a[1], o[1])

    def scan(o, d0, d1, init, op0, op1):
        emit("V", lambda: g.vector.tensor_tensor_scan(o[0], d0[0], d1[0], init, op0, op1), d0[1] + d1[1], o[1])

    def fill(o, c):
        emit("V", lambda: g.vector.memset(o[0], c), [], o[1])

    def act(o, a, func, bias=None, scale=1.0, acc=None):
        r, w, kw = list(a[1]), list(o[1]), {"scale": scale}
        if bias is not None:
            kw["bias"] = bias[0]
            r += bias[1]
        if acc is not None:
            kw["accum_out"] = acc[0]
            w += acc[1]
        emit("S", lambda: g.scalar.activation(o[0], a[0], func, **kw), r, w)

    def quant(name, src, n, a=0):
        q, s = v("q" + name, a, a + n), v("s" + name, a, a + n)
        emit("V", lambda: g.vector.quantize_mx(q[0], s[0], src[0]), src[1], q[1] + s[1])

    def mm(bank, n, l, la, r, ra=0):
        o = ps(bank, n)
        lq, ls = v("q" + l, la, la + 128), v("s" + l, la, la + 128)
        rq, rs = v("q" + r, ra, ra + n), v("s" + r, ra, ra + n)
        emit("P", lambda: g.tensor.matmul_mx(o[0], lq[0], ls[0], rq[0], rs[0], True, True), lq[1] + ls[1] + rq[1] + rs[1], o[1])

    def iota(o, pattern, base=0, cm=0, small=True):
        if small:
            emit("G", lambda: g.iota(o[0], pattern, base, cm, allow_small_or_imprecise_dtypes=True), [], o[1])
        else:
            emit("G", lambda: g.iota(o[0], pattern, base, cm), [], o[1])

    def keep_where(o, pattern, op, base, cm):
        emit("G", lambda: g.affine_select(o[0], o[0], pattern, op, 0.0, base, cm), o[1], o[1])

    dma("Y", T.xin[:], T.x[:], [], v("xin")[1])
    dma("S", T.uin[:], T.u[:], [], v("uin")[1])
    dma("Y", T.nmi[:], T.nm[:], [], v("nmi")[1])
    dma("S", T.hin[:], T.h[:], [], v("hin")[1])
    dma("Y", T.qw[:, 0:512].bitcast(dt.uint8), T.wc[:, 0:2048], [], v("qw")[1])
    dma("S", T.sw[:], T.ws[:], [], v("sw")[1])
    dma("Y", T.vin[:], T.v[:], [], v("vin")[1])

    iota(v("qi"), [[0, 1]], 0, 1, small=False)
    iota(v("o16"), [[1, 16]])
    fill(v("blk"), 1.0)
    fill(v("tmpl", 0, 240), 1.0)
    fill(v("tmpl", 256, 257), 2048.0)
    keep_where(v("blk"), [[-16, 8], [0, 16]], A.is_ge, 0, 1)
    keep_where(v("blk"), [[16, 8], [0, 16]], A.is_ge, 15, -1)
    iota(v("r16"), [[0, 16], [1, 16]])
    emit("V", lambda: g.vector.tensor_scalar(T.qi2[:], T.qi[:], 15, None, A.bitwise_and), v("qi")[1], v("qi2")[1])
    cp(v("kap"), v("qi2"))
    fill(v("inc", 0, 1), 2048.0)
    ts(v("own1"), v("o16"), v("kap"), A.is_lt)
    ts(v("own2"), v("o16"), v("kap"), A.is_equal, -256.0, A.mult)
    ts(v("pe16"), v("o16"), v("kap"), A.is_lt, 1.0, A.add)
    tt(v("tmpl", 240, 256), v("own1"), v("own2"), A.add)
    scan(v("pwv"), v("pe16"), v("pe16"), 1.0, A.mult, A.max)
    fill(v("ntile"), 0.0)
    for m in range(15, -1, -1):
        n = 16 * m + 15 + (m < 15)
        act(v("inc", off1(m) + 1, off1(m) + 1 + n), v("tmpl", 241 - 16 * m, 241 - 16 * m + n), F.Copy)
    ts(v("pw"), v("kap"), 6.5, A.is_lt, v("pwv", 15, 16), A.mult)
    fill(v("bits"), 0.0)
    iota(v("im"), [[1, 16]], 0, 0, small=False)
    iota(v("base0"), [[16, 16]], -257)
    iota(v("plc"), [[1, 128]], 1)
    iota(v("plcr"), [[-1, 128]], 128)
    fill(v("idn"), HALF)
    keep_where(v("idn"), [[-1, 128]], A.is_equal, 0, 1)
    iota(v("ctile"), [[0, 2048]])
    iota(v("iota"), [[1, 384]], -128)
    iota(v("iotap"), [[1, 256]])
    iota(v("keep2", 256, S2), [[0, S2 - 256]], 1)
    iota(v("sc2", S2, S2 + 16), [[512, 16]])
    iota(v("zeros"), [[0, 256]])
    iota(v("alive0"), [[0, 384]], 1)
    iota(v("ones"), [[0, 384]], 1)
    iota(v("thr0"), [[16, 8]])
    iota(v("c2"), [[32, 8]], 272)
    iota(v("c2l"), [[-32, 8]], 496)
    for i in range(1, R):
        iota(v("alive%d" % i), [[0, 384]], 1)
    ts(v("ntile", 0, 512, 4), v("blk"), v("pw"), A.mult)
    ts(v("ntile", 513, 1024, 4), v("blk"), v("pw"), A.mult)
    quant("n", v("ntile"), 256)
    quant("u", v("uin"), 128)
    ts(v("diag"), v("r16"), v("kap"), A.is_equal)
    for hf in (0, 1):
        quant("x0", v("xin", 512 * hf, 512 * hf + 512), 128, 128 * hf)
        mm(hf, 128, "u", 0, "x0", 128 * hf)
    ts(v("keep"), v("r16"), 0.0, A.not_equal)

    def x_of(t, b, a=0, e=256):
        return v("gx" if t == 0 else "g%d" % (t - 1), 384 * b + 128 + a, 384 * b + 128 + e)

    def front_of(t, b):
        return v("g%d" % t, 384 * b, 384 * b + 128)

    def decode_x(t, planes):
        for b in planes:
            mm(4 + b, 256, "e", 128 * b, "x%d" % t)

    def copy_x(t, planes, q="S"):
        for b in planes:
            if q == "S":
                act(x_of(t, b), ps(4 + b, 256), F.Copy)
            else:
                cp(x_of(t, b), ps(4 + b, 256))

    def decode_f(t):
        for b in range(4):
            mm(b, 128, "e", 128 * b, "f%d" % t)
            act(front_of(t, b), ps(b, 128), F.Copy)

    def names_in(t):
        p = "plcr" if t else "plc"
        emit("V", lambda: g.vector.tensor_copy(T["pt%d" % t][:, 0:128].indirect(T["la%d" % t][:, 0:8]), T[p][:]),
             v(p)[1] + v("la%d" % t)[1], v("pt%d" % t)[1])

    def names_row(t):
        act(v("trw%d" % t, 0, 128), ind(v("iotap", 0, 128), v("la%d" % t)), F.Copy)

    nxt = T.cores[(rank + 1) % len(T.cores)]
    rid, pid = topo.addr(nxt, core)
    eng = topo.engines(core, nxt)[:8]
    mask = sum(1 << e for e in eng)

    def send(dst, src, rsem, reads):
        wait("G", need_of("G", reads, []))
        g.remote_dma(dst, src, T.sem[rsem], T.sem.left, pid, rid, mask)
        left[0] += len(eng)

    def send_names(t):
        send(T["la%d" % (t + 1)][:], T["sa%d" % t][:], "ra%d" % t, v("sa%d" % t)[1])
        hist["la%d" % (t + 1)] = [(0, 8, True, "R", "ra%d" % t, len(eng))]

    def border_send(t):
        quant("b%d" % t, v("bt%d" % t), 128)
        send(T["qf%d" % (t + 1)][:, 0:128].bitcast(dt.uint8), T["qb%d" % t][:, 0:128].bitcast(dt.uint8), "rb%d" % t, v("qb%d" % t)[1])
        send(T["sf%d" % (t + 1)][:], T["sb%d" % t][:], "rb%d" % t, v("sb%d" % t)[1])
        for n in ("qf%d", "sf%d"):
            hist[n % (t + 1)] = [(0, 128, True, "R", "rb%d" % t, 2 * len(eng))]

    def border_alive(t):
        emit("V", lambda: g.vector.tensor_copy(T["alive%d" % t][:, 0:384].indirect(T.v16[:, 0:16]), T.zeros[:]),
             v("zeros")[1] + v("v16")[1] + v("alive%d" % t)[1], v("alive%d" % t)[1])
        scan(v("arow"), v("ones"), v("alive%d" % t), 0.0, A.mult, A.add)

    def junk(n):
        turn[0] = (turn[0] + 1) % 4
        return v("junk", 384 * turn[0], 384 * turn[0] + n)

    def border_count(t, ms, q="S"):
        last = t == R - 1
        thr = "thrl" if last else "thr"
        for m in ms:
            a = 112 - 16 * m if last else 16 * m
            if q == "S":
                act(junk(272), v("arow", a, a + 272), F.Sign, bias=v(thr, m, m + 1), scale=-1.0, acc=v("accb", m, m + 1))
            else:
                turn[1] = (turn[1] + 1) % 3
                o = v("ltb", 272 * turn[1], 272 * turn[1] + 272)
                ts(o, v("arow", a, a + 272), v(thr, m, m + 1), A.is_lt, 2.0, A.mult)
                scan(v("cs", 272 * m, 272 * m + 272), v("ones", 0, 272), o, -272.0, A.mult, A.add)

    def border_columns(t):
        n, c2 = (NLAST, "c2l") if t == R - 1 else (NMID, "c2")
        yield tt(v("sb_", n, 8), v("cs", 272 * n + 271, 2176, 272), v(c2, n, 8), A.add)
        yield tt(v("sb_", 0, n), v("accb", 0, n), v(c2, 0, n), A.add)
        if t == 0:
            yield ts(v("sa_"), v("sb_"), 255.5, A.is_ge, 0.5, A.mult)
            yield ts(v("sc_"), v("sb_"), -0.5, A.mult, 127.0, A.add)
            yield tt(v("sa_"), v("sa_"), v("sb_"), A.mult)
            yield tt(v("sf_"), v("sa_"), v("sc_"), A.max)
            yield cp(v("src16"), v("sf_"))
        else:
            yield ts(v("src16"), v("sb_"), 0.5, A.mult)

    def border_names(t):
        yield tt(v("mn"), ind(v("trw%d" % t), v("src16")), v("diag", 0, 128), A.mult)
        yield scan(v("mh"), v("keep", 0, 128), v("mn"), 0.0, A.mult, A.add)
        yield cp(v("sa%d" % t), v("mh", 15, 128, 16))
        send_names(t)

    def border_list(t):
        yield from border_columns(t)
        yield from border_names(t)

    def border_gather(t, b, q):
        o, i = v("bt%d" % t, b, 512, 4), ind(v("g%d" % t, 384 * b, 384 * b + 384), v("src16"))
        if q == "S":
            act(o, i, F.Copy, scale=2.0)
        else:
            ts(o, i, 2.0, A.mult)

    for t in range(R):
        tr = "trw%d" % t
        ts(v("bits", 0, 512, 4), ps(0, 128), 0.0, A.is_lt)
        ts(v("bits", 1, 512, 4), ps(1, 128), 0.0, A.is_lt)
        quant("bit", v("bits"), 128)
        mm(2, 128, "n", 0, "bit")
        mm(3, 128, "n", 128, "bit")
        if t > 0:
            decode_x(t, range(4))
            border_count(t - 1, range(NMID, 8), "V")
        else:
            cp(v("la0"), v("nmi"))
            names_in(0)
            cp(v("lm"), v("im"))
        for hf in (0, 1):
            a, e = 128 * hf, 128 * hf + 128
            tt(v("hm", a, e), ps(2 + hf, 128), v("diag", a, e), A.mult)
            act(v(tr, 128 + a, 128 + e), ps(2 + hf, 128), F.Copy)
        if t > 0:
            border_count(t - 1, range(NEARLY, NMID))
        scan(v("hold"), v("keep"), v("hm"), 0.0, A.mult, A.add)
        if t == 0:
            for b in range(4):
                act(v("ctile", 512 * b + b, 512 * b + 512, 4), v("idn"), F.Copy)
            ts(v("base"), v("base0"), v("kap"), A.add)
            ts(v("k1"), v("kap"), 1.5, A.add)
            ts(v("e1"), v("kap"), 16.0 * MS + 16.0, A.mult, 255.0 - 16.0 * MS, A.add)
            ts(v("e3"), v("kap"), -16.0 * MS, A.mult, 255.0 + 16.0 * MS * MS, A.add)
            ts(v("e2"), v("kap"), float(S2), A.add)
            ts(v("sel1"), v("kap"), 0.5, A.is_ge)
            tt(v("k2"), v("k1"), v("k1"), A.mult)
            tt(v("pe"), v("e1"), v("e3"), A.min)
            ts(v("sel2"), v("kap"), MS - 0.5, A.is_lt, v("sel1"), A.mult)
            ts(v("ends"), v("k2"), 8.0, A.mult, -3.0, A.add)
            ts(v("pr"), v("pe"), v("e2"), A.subtract, v("sel2"), A.mult)
            fill(v("bm64"), -64.0)
            ts(v("ends2"), v("pr"), v("e2"), A.add)
        else:
            copy_x(t, range(4))
        steps = border_list(t - 1) if t > 0 else iter(())
        for m in range(16):
            ts(v("qq", off1(m), off1(m + 1)), v(tr, 128, 144 + 16 * m), v("hold", 16 * m + 15, 16 * m + 16), A.not_equal, 1024.0, A.mult)
            if m >= LSTEP:
                next(steps, None)
        cp(v("nw16"), v("hold", 15, 256, 16))
        for x in steps:
            pass
        if t == 0:
            quant("f0", v("hin"), 128)
        else:
            for b in range(4):
                border_gather(t - 1, b, "S")
        scan(v("sc"), v("inc"), v("qq"), 0.0, A.add, A.min)
        if t > 0:
            border_send(t - 1)
        else:
            quant("e", v("ctile"), 512)
            decode_x(0, range(4))
            copy_x(0, range(4))
        ts(v("nh"), ind(v("sc"), v("ends")), -0.5, A.is_ge, 1024.0, A.mult)
        tt(v("x1"), ind(v("sc"), v("ends")), v("base"), A.subtract)
        if t > 0:
            names_in(t)
        names_row(t)
        tt(v("pl"), ind(v("pt%d" % t), v("nw16")), v("diag"), A.mult)
        tt(v("w1"), v("x1"), v("nh"), A.add)
        scan(v("plh"), v("keep"), v("pl"), 0.0, A.mult, A.add)
        tt(v("w"), v("w1"), v("plh", 15, 256, 16), A.min)
        ts(v("v16"), v("w"), -1.0, A.mult, 128.0, A.add)
        act(v("vw"), v("w"), F.Copy, scale=-1.0)
        act(v("e32", 0, 16), v("w"), F.Identity, bias=v("bm64"), scale=64.0)
        cp(v("vr"), ind(v("iota"), v("v16")))
        if t == 0:
            ts(v("keep2", 0, 256), v("diag"), 63.0, A.mult, 1.0, A.add)
            fill(v("keep2", 0, 256, 16), 0.0)
            fill(v("keep2", 256, S2, 16 * MS), 0.0)
            fill(v("keep2", 272, S2, 16 * MS + 16), 0.0)
        for m in range(MS, 16):
            act(junk(16 * m), v("vr", 0, 16 * m), F.Sign, bias=v("vw", m, m + 1), scale=-1.0, acc=v("acc", m, m + 1))
        act(v("e32", 16 + MS, 32), v("acc", MS, 16), F.Copy, scale=32.0)

        def shorter(a, b):
            for m in range(a, b):
                ts(v("lt", off2(m), off2(m) + 16 * m), v("vr", 0, 16 * m), v("vw", m, m + 1), A.is_lt, 64.0, A.mult)

        tt(v("lt", 0, 256), ind(v("vw"), v("lm")), v("vr"), A.is_gt)
        shorter(1, 4)
        scan(v("sc2", 0, 256), v("keep2", 0, 256), v("lt", 0, 256), 0.0, A.mult, A.add)
        shorter(4, MS)
        tt(v("dd"), v("sc2", 15, 256, 16), v("e32", 0, 16), A.add)
        scan(v("sc2", 256, S2), v("keep2", 256, S2), v("lt", 256, S2), 0.0, A.mult, A.add)
        tt(v("dd", MS, 16), v("dd", MS, 16), v("e32", 16 + MS, 32), A.add)
        tt(v("d"), ind(v("sc2"), v("ends2")), v("dd"), A.add)
        if t == 0:
            ts(v("d16"), v("d"), 1.0 / 64, A.mult)
        else:
            ts(v("d16"), v("d"), -1.0 / 64, A.mult, 127.0, A.add)
        decode_f(t)
        for hf in (0, 1):
            a, e = 128 * hf, 128 * hf + 128
            for b in range(4):
                tt(v("zt", 4 * a + b, 4 * e, 4), ind(front_of(t, b), v("d16", 8 * hf, 8 * hf + 8)), x_of(t, b, a, e), A.add)
            quant("z", v("zt", 4 * a, 4 * e), 128, a)
            for b in range(4):
                mm(4 * hf + b, 128, "w", 128 * b, "z", a)
        if t == 0:
            ts(v("thr"), v("thr0"), v("kap"), A.add, 0.5, A.add)
        border_alive(t)
        if t == 0:
            ts(v("thrl"), v("thr"), -1.0, A.mult, 128.0, A.add)
            fill(v("b127"), 127.0)
        for hf in (0, 1):
            a, e = 128 * hf, 128 * hf + 128
            for b in range(4):
                if hf == 1 and b >= YV:
                    ts(v("yt", 4 * a + b, 4 * e, 4), ps(4 * hf + b, 128), 0.03125, A.mult)
                else:
                    act(v("yt", 4 * a + b, 4 * e, 4), ps(4 * hf + b, 128), F.Copy, scale=0.03125)
            quant("x%d" % (t + 1), v("yt", 4 * a, 4 * e), 128, a)
            if t < R - 1:
                mm(hf, 128, "u", 0, "x%d" % (t + 1), a)
        if t < R - 1:
            border_count(t, range(NEARLY))

    decode_x(R, range(4))
    border_count(R - 1, range(NLAST))
    border_count(R - 1, range(NLAST, 7), "V")
    copy_x(R, (0, 1, 3))
    copy_x(R, (2,), "V")
    border_count(R - 1, (7,), "V")
    for x in border_columns(R - 1):
        pass
    for b in (0, 1):
        border_gather(R - 1, b, "S")
    for b in (2, 3):
        border_gather(R - 1, b, "V")
    border_send(R - 1)
    for x in border_names(R - 1):
        pass
    quant("v", v("vin"), 128)
    mm(1, 256, "v", 0, "x3")
    act(v("ysb", 0, 256), ps(1, 256), F.Copy)
    act(v("olb", 0, 256), ind(v("iotap"), v("d16")), F.Identity, bias=v("b127"), scale=-1.0)

    def stores(a, n, q, s):
        dma("Y", T.oc[:, 4 * a:4 * (a + n)], T[q][:, 0:n].bitcast(dt.uint8), v(q)[1], [])
        for k in range(4):
            dma("Y" if k % 2 else "S", T.osc[4 * k:4 * k + 4, a:a + n], T[s][32 * k:32 * k + 4, 0:n], v(s)[1], [])

    dma("S", T.y[:, 0:256], T.ysb[:, 0:256], v("ysb", 0, 256)[1], [])
    stores(0, 256, "qx3", "sx3")
    mm(2, 128, "v", 0, "f3")
    cp(v("ysb", 256, 384), ps(2, 128))
    stores(256, 128, "qf3", "sf3")
    dma("Y", T.y[:, 256:384], T.ysb[:, 256:384], v("ysb", 256, 384)[1], [])
    act(v("olb", 256, 384), ind(v("iotap"), v("la3")), F.Copy)
    dma("S", T.ol[:, :], T.olb[0:128:16, :], v("olb")[1], [])

    for s in ("cv", "cs", "cp", "cg"):
        g.wait_ge(T.sem[s], count[s])
    for i in range(dmas[0]):
        g.wait_ge(T.sem["d%d" % i], 16)
    for i in range(R):
        g.wait_ge(T.sem["ra%d" % i], len(eng))
        g.wait_ge(T.sem["rb%d" % i], 2 * len(eng))
    g.wait_ge(T.sem.left, left[0])
